import numpy as np
import ml_dtypes


def mxq(x, axis, fmt="e4m3"):
    dtype, down = {"e4m3": (ml_dtypes.float8_e4m3fn, 7), "e5m2": (ml_dtypes.float8_e5m2, 14)}[fmt]
    v = np.moveaxis(np.asarray(x, np.float32).astype(ml_dtypes.bfloat16).astype(np.float64), axis, -1)
    blocks = v.reshape(v.shape[:-1] + (-1, 32))
    amax = np.abs(blocks).max(-1, keepdims=True)
    byte = np.maximum(np.where(amax > 0, np.frexp(amax)[1] - 1 + 127, 0) - down, 1)
    scale = np.exp2(byte - 127.0)
    codes = (blocks / scale).astype(np.float32).astype(dtype).astype(np.float64)
    return np.moveaxis((codes * scale).reshape(v.shape), -1, axis)


WIDE = False


def mx_kscale(k):
    if not WIDE:
        return np.ones(k)
    levels = np.array([10, -10, 5, -5, 0])
    if k % 512:
        return np.exp2(np.random.permutation(np.resize(levels, k // 32))).repeat(32)
    a = np.empty((k // 512, 16))
    for p in range(k // 512):
        a[p, :8] = np.random.permutation(np.resize(levels, 8))
        for g in range(8):
            far = levels[np.abs(levels - a[p, g]) >= 10]
            a[p, g + 8] = far[np.random.randint(len(far))]
    return np.exp2(a.ravel()).repeat(32)


def f64(x):
    return np.asarray(x).astype(np.float64)


def striped(idx):
    return np.tile(idx.reshape(-1, 16).T, (8, 1)).astype(np.uint16)


def unstriped(offs):
    return offs[:16].T.reshape(-1).astype(np.int64)


E2M1 = np.array([0.0, 0.5, 1.0, 1.5, 2.0, 3.0, 4.0, 6.0, -0.0, -0.5, -1.0, -1.5, -2.0, -3.0, -4.0, -6.0])


def pack_weight(w, fmt):
    k, n = w.shape
    w = f64(np.asarray(w, np.float32).astype(ml_dtypes.bfloat16)).reshape(k // 32, 32, n)
    amax = np.abs(w).max(1)
    if fmt == "e4m3":
        byte = np.frexp(amax)[1] - 1 + 127 - 7
    else:
        mant, ex = np.frexp(amax / 6.0)
        byte = np.where(mant > 0.5, ex, ex - 1) + 127
    byte = np.clip(np.where(amax > 0, byte, 1), 1, 254)
    scaled = (w * np.exp2(127.0 - byte)[:, None, :]).reshape(k, n).astype(np.float32)
    by_word = np.ascontiguousarray(scaled.reshape(k // 512, 128, 4, n).transpose(0, 1, 3, 2))
    if fmt == "e4m3":
        words = by_word.astype(ml_dtypes.float8_e4m3fn).view(np.uint8)
    else:
        c = by_word.astype(ml_dtypes.float4_e2m1fn).view(np.uint8) & 0xF
        words = (c[..., 0::2] | (c[..., 1::2] << 4)).reshape(k // 512, 128, 2 * n)
    return np.ascontiguousarray(words), np.ascontiguousarray(byte.astype(np.uint8).reshape(k // 512, 16, n))


def unpack_weight(words, scales, fmt):
    g, _, n = scales.shape
    words = np.ascontiguousarray(words).reshape(g, 128, n, -1)
    if fmt == "e4m3":
        vals = words.view(ml_dtypes.float8_e4m3fn).astype(np.float64)
    else:
        nib = np.empty((g, 128, n, 4), np.uint8)
        nib[..., 0::2] = words & 0xF
        nib[..., 1::2] = words >> 4
        vals = E2M1[nib]
    vals = vals * np.repeat(np.exp2(scales.astype(np.float64) - 127.0), 8, axis=1)[..., None]
    return vals.transpose(0, 1, 3, 2).reshape(g * 512, n)


def gelu(v):
    return 0.5 * v * (1.0 + np.tanh(np.sqrt(2.0 / np.pi) * (v + 0.044715 * v**3)))


K, T, E, B, H, N = 512, 512, 4, 4, 512, 256


def setup_inputs():
    n = np.random.standard_normal
    s = mx_kscale(K)
    u = mx_kscale(H)
    slot_token = np.random.permutation(T)[:128 * B]
    block = np.sort(np.random.randint(E, size=B))
    x = pack_weight(n((K, T)) * s[:, None], "e4m3")
    w = pack_weight(n((K, N)) / np.sqrt(K) / s[:, None], "e2m1")
    wa = pack_weight(n((K, E * H)) / np.sqrt(K) / s[:, None] * np.tile(u, E), "e4m3")
    wb = pack_weight(n((H, E * N)) / np.sqrt(H) / u[:, None], "e4m3")
    return {
        "x_words": x[0],
        "x_scales": x[1],
        "w_words": w[0],
        "w_scales": w[1],
        "wa_words": wa[0],
        "wa_scales": wa[1],
        "wb_words": wb[0],
        "wb_scales": wb[1],
        "gate": (np.tile(np.random.uniform(0.2, 1.0, 128 * B), (128, 1))).astype(np.float32),
        "offs": striped(slot_token),
        "offs2": striped((block[:, None] * H + np.arange(H)).reshape(-1)),
        "offs3": striped((block[:, None] * N + np.arange(N)).reshape(-1)),
    }


def reference(x_words, x_scales, w_words, w_scales, wa_words, wa_scales, wb_words, wb_scales, gate, offs, offs2, offs3):
    w = unpack_weight(w_words, w_scales, "e2m1")
    idx, idx2, idx3 = unstriped(offs), unstriped(offs2), unstriped(offs3)
    x = unpack_weight(x_words, x_scales, "e4m3")
    out = w.T @ x
    wa = unpack_weight(wa_words, wa_scales, "e4m3")[:, idx2]
    wb = unpack_weight(wb_words, wb_scales, "e4m3")[:, idx3]
    xq = x[:, idx]
    h = np.concatenate([wa[:, m * H:(m + 1) * H].T @ xq[:, 128 * m:128 * m + 128] for m in range(B)], axis=1)
    hq = mxq(gelu(h), 0, "e4m3")
    y = np.concatenate([wb[:, m * N:(m + 1) * N].T @ hq[:, 128 * m:128 * m + 128] for m in range(B)], axis=1)
    out[:, idx] += f64(gate[:1]) * y
    return out

@@ -1,0 +1,161 @@
+from contextlib import ExitStack
+
+import concourse.mybir as mybir
+from concourse.masks import make_identity
+
+K, T, E, B, H, N = 512, 512, 4, 4, 512, 256
+P = 128
+FLOPS = 2 * K * N * T + 2 * K * H * T + 2 * H * N * T
+
+F32 = mybir.dt.float32
+BF16 = mybir.dt.bfloat16
+I32 = mybir.dt.int32
+U32 = mybir.dt.uint32
+U16 = mybir.dt.uint16
+U8 = mybir.dt.uint8
+FP8X4 = mybir.dt.float8_e4m3fn_x4
+FP4X4 = mybir.dt.float4_e2m1fn_x4
+GELU = mybir.ActivationFunctionType.Gelu_apprx_tanh
+MULT = mybir.AluOpType.mult
+ADD = mybir.AluOpType.add
+
+WA_ROW = 4
+WB_ROW = 8
+
+
+def tile_moe_dyl_gelu_kernel(
+    tc, x_words, x_scales, w_words, w_scales, wa_words, wa_scales, wb_words, wb_scales, gate, offs, offs2, offs3, out
+):
+    nc = tc.nc
+    with ExitStack() as ctx:
+        keep = ctx.enter_context(tc.tile_pool(name="keep", bufs=1))
+        ps_h = ctx.enter_context(tc.psum_pool(name="ps_h", bufs=2))
+        ps_t = ctx.enter_context(tc.psum_pool(name="ps_t", bufs=2))
+        ps_keep = ctx.enter_context(tc.psum_pool(name="ps_keep", bufs=1))
+
+        def sb(name, cols, dtype):
+            return keep.tile([P, cols], dtype, name=name, align_bytes=64)
+
+        tok_list = sb("tok_list", T // 16, U16)
+        wa_list = sb("wa_list", B * H // 16, U16)
+        wb_list = sb("wb_list", B * N // 16, U16)
+        xw, xs = sb("xw", T, I32), sb("xs", T, U8)
+        waw, was = sb("waw", E * H, I32), sb("was", E * H, U8)
+        wbw, wbs = sb("wbw", E * N, I32), sb("wbs", E * N, U8)
+        ww, ws = sb("ww", 2 * N, U8), sb("ws", N, U8)
+        gate_sb = sb("gate_sb", T, F32)
+        xw_g, xs_g = sb("xw_g", T, U32), sb("xs_g", T, U8)
+        waw_g, was_g = sb("waw_g", B * H, U32), sb("was_g", B * H, U8)
+        wbw_g, wbs_g = sb("wbw_g", B * N, U32), sb("wbs_g", B * N, U8)
+        ident = sb("ident", P, F32)
+        h_rows = sb("h_rows", B * H, BF16)
+        h_cols = sb("h_cols", B * H, BF16)
+        hq, hs = sb("hq", T, U32), sb("hs", T, U8)
+        y_sb = [sb("y_sb%d" % c, T, F32) for c in range(2)]
+        placed = [sb("placed%d" % c, T, F32) for c in range(2)]
+        res = [sb("res%d" % c, T, F32) for c in range(2)]
+        y_ps = [ps_keep.tile([P, T], F32, name="y_ps%d" % c) for c in range(2)]
+        base_ps = [ps_keep.tile([P, T], F32, name="base_ps%d" % c) for c in range(2)]
+
+        def load_words(tile, words):
+            nc.sync.dma_start(out=tile[:], in_=words[0].rearrange("p c d -> p (c d)").bitcast(I32))
+
+        def load_scales(tile, scales, row):
+            for r in range(4):
+                nc.sync.dma_start(out=tile[row + r : P : 32, :].bitcast(I32), in_=scales[0, r:16:4, :].bitcast(I32))
+
+        def gather(dst, window, lst, lo, hi):
+            nc.vector.tensor_copy(out=dst[:, lo:hi], in_=window.indirect(lst[:, lo // 16 : hi // 16]))
+
+        for plane in (was, xs, wbs, ws):
+            nc.vector.memset(plane[:].bitcast(I32), 0)
+        nc.vector.memset(ident[:], 0.0)
+        make_identity(nc, ident[:], nomemset=True)
+
+        load_words(xw, x_words)
+        nc.sync.dma_start(tok_list[:], offs)
+        nc.sync.dma_start(wa_list[:], offs2)
+        load_scales(was, wa_scales, WA_ROW)
+        load_words(waw, wa_words)
+        load_scales(xs, x_scales, 0)
+        nc.sync.dma_start(wb_list[:], offs3)
+        load_words(wbw, wb_words)
+        load_scales(wbs, wb_scales, WB_ROW)
+        nc.sync.dma_start(out=gate_sb[:], in_=gate)
+        nc.sync.dma_start(out=ww[:].bitcast(I32), in_=w_words[0].bitcast(I32))
+        load_scales(ws, w_scales, 0)
+
+        def first_layer(m):
+            slots = slice(P * m, P * m + P)
+            inner = slice(H * m, H * m + H)
+            h_ps = ps_h.tile([P, H], F32, name="h_ps")
+            nc.tensor.matmul_mx(
+                out=h_ps[:],
+                lhsT=xw_g[:, slots].bitcast(FP8X4), lhsT_scale=xs_g[:, slots],
+                rhs=waw_g[:, inner].bitcast(FP8X4), rhs_scale=was_g[WA_ROW:P, inner],
+                start=True, stop=True,
+            )
+            nc.scalar.activation(
+                out=h_rows[:, inner].rearrange("s (u p e) -> s u p e", u=2, e=2),
+                in_=h_ps[:].rearrange("s (p u e) -> s u p e", u=2, e=2),
+                func=GELU,
+            )
+            pairs = h_rows[:, inner].bitcast(F32)
+            t_ps = ps_t.tile([P, 2, P], F32, name="t_ps")
+            for u in range(2):
+                nc.tensor.transpose(t_ps[:, u, :], pairs[:, P * u : P * u + P], ident[:])
+            nc.scalar.copy(
+                out=h_cols[:, inner].bitcast(F32).rearrange("p (s u) -> p s u", u=2),
+                in_=t_ps[:].rearrange("p u s -> p s u"),
+            )
+
+        def second_layer(m0, m1):
+            slots = slice(P * m0, P * m1)
+            nc.vector.quantize_mx(out=hq[:, slots].bitcast(FP8X4), scales=hs[:, slots], in_=h_cols[:, H * m0 : H * m1])
+            for c in range(2):
+                for m in range(m0, m1):
+                    blk = slice(P * m, P * m + P)
+                    cols = slice(N * m + P * c, N * m + P * c + P)
+                    nc.tensor.matmul_mx(
+                        out=y_ps[c][:, blk],
+                        lhsT=wbw_g[:, cols].bitcast(FP8X4), lhsT_scale=wbs_g[WB_ROW:P, cols],
+                        rhs=hq[:, blk].bitcast(FP8X4), rhs_scale=hs[:, blk],
+                        start=True, stop=True,
+                    )
+                nc.scalar.copy(out=y_sb[c][:, slots], in_=y_ps[c][:, slots])
+
+        def scatter(c, lo, hi):
+            nc.vector.tensor_tensor(
+                out=placed[c][:].indirect(tok_list[:, lo // 16 : hi // 16]),
+                in0=y_sb[c][:, lo:hi], in1=gate_sb[:, lo:hi], op=MULT,
+            )
+
+        half = T // 2
+        for lo in (0, half):
+            gather(xw_g, xw[:].bitcast(U32), tok_list, lo, lo + half)
+        for lo in (0, 2 * H):
+            gather(was_g, was[:], wa_list, lo, lo + 2 * H)
+        gather(waw_g, waw[:].bitcast(U32), wa_list, 0, H)
+        for lo in (0, half):
+            gather(xs_g, xs[:], tok_list, lo, lo + half)
+        first_layer(0)
+        for m in range(1, B):
+            gather(waw_g, waw[:].bitcast(U32), wa_list, H * m, H * m + H)
+            first_layer(m)
+        for m0 in (0, 2):
+            gather(wbw_g, wbw[:].bitcast(U32), wb_list, N * m0, N * m0 + 2 * N)
+            gather(wbs_g, wbs[:], wb_list, N * m0, N * m0 + 2 * N)
+            second_layer(m0, m0 + 2)
+        for c in range(2):
+            nc.tensor.matmul_mx(
+                out=base_ps[c][:],
+                lhsT=ww[:, 2 * P * c : 2 * P * c + 2 * P].bitcast(FP4X4), lhsT_scale=ws[:, P * c : P * c + P],
+                rhs=xw[:].bitcast(FP8X4), rhs_scale=xs[:],
+                start=True, stop=True,
+            )
+        for lo in (0, half):
+            for c in range(2):
+                scatter(c, lo, lo + half)
+        for c in range(2):
+            nc.vector.tensor_tensor(out=res[c][:], in0=base_ps[c][:], in1=placed[c][:], op=ADD)
+            nc.sync.dma_start(out=out[P * c : P * c + P, :], in_=res[c][:])

@@ -21,6 +21,7 @@ ADD = mybir.AluOpType.add
 
 WA_ROW = 4
 WB_ROW = 8
+WA_FIRST = 1920
 
 
 def tile_moe_dyl_gelu_kernel(
@@ -29,12 +30,13 @@ def tile_moe_dyl_gelu_kernel(
     nc = tc.nc
     with ExitStack() as ctx:
         keep = ctx.enter_context(tc.tile_pool(name="keep", bufs=1))
-        ps_h = ctx.enter_context(tc.psum_pool(name="ps_h", bufs=2))
-        ps_t = ctx.enter_context(tc.psum_pool(name="ps_t", bufs=2))
-        ps_keep = ctx.enter_context(tc.psum_pool(name="ps_keep", bufs=1))
+        psum = ctx.enter_context(tc.psum_pool(name="psum", bufs=1))
 
-        def sb(name, cols, dtype):
-            return keep.tile([P, cols], dtype, name=name, align_bytes=64)
+        def sb(name, cols, dtype, slot=None):
+            return keep.tile([P, cols], dtype, name=name, tag=slot or name, align_bytes=64)
+
+        def bank(name, slot):
+            return psum.tile([P, 512], F32, name=name, tag=slot)
 
         tok_list = sb("tok_list", T // 16, U16)
         wa_list = sb("wa_list", B * H // 16, U16)
@@ -44,118 +46,170 @@ def tile_moe_dyl_gelu_kernel(
         wbw, wbs = sb("wbw", E * N, I32), sb("wbs", E * N, U8)
         ww, ws = sb("ww", 2 * N, U8), sb("ws", N, U8)
         gate_sb = sb("gate_sb", T, F32)
-        xw_g, xs_g = sb("xw_g", T, U32), sb("xs_g", T, U8)
-        waw_g, was_g = sb("waw_g", B * H, U32), sb("was_g", B * H, U8)
-        wbw_g, wbs_g = sb("wbw_g", B * N, U32), sb("wbs_g", B * N, U8)
         ident = sb("ident", P, F32)
-        h_rows = sb("h_rows", B * H, BF16)
-        h_cols = sb("h_cols", B * H, BF16)
-        hq, hs = sb("hq", T, U32), sb("hs", T, U8)
-        y_sb = [sb("y_sb%d" % c, T, F32) for c in range(2)]
         placed = [sb("placed%d" % c, T, F32) for c in range(2)]
         res = [sb("res%d" % c, T, F32) for c in range(2)]
-        y_ps = [ps_keep.tile([P, T], F32, name="y_ps%d" % c) for c in range(2)]
-        base_ps = [ps_keep.tile([P, T], F32, name="base_ps%d" % c) for c in range(2)]
 
-        def load_words(tile, words):
-            nc.sync.dma_start(out=tile[:], in_=words[0].rearrange("p c d -> p (c d)").bitcast(I32))
+        def load_words(tile, words, lo, hi):
+            nc.sync.dma_start(out=tile[:, lo:hi], in_=words[0, :, lo:hi, :].rearrange("p c d -> p (c d)").bitcast(I32))
 
-        def load_scales(tile, scales, row):
-            for r in range(4):
+        def load_scales(tile, scales, row, rows=range(4)):
+            for r in rows:
                 nc.sync.dma_start(out=tile[row + r : P : 32, :].bitcast(I32), in_=scales[0, r:16:4, :].bitcast(I32))
-
-        def gather(dst, window, lst, lo, hi):
-            nc.vector.tensor_copy(out=dst[:, lo:hi], in_=window.indirect(lst[:, lo // 16 : hi // 16]))
 
         for plane in (was, xs, wbs, ws):
             nc.vector.memset(plane[:].bitcast(I32), 0)
         nc.vector.memset(ident[:], 0.0)
-        make_identity(nc, ident[:], nomemset=True)
 
-        load_words(xw, x_words)
+        make_identity(nc, ident[:], nomemset=True)
+        load_words(xw, x_words, 0, T)
         nc.sync.dma_start(tok_list[:], offs)
         nc.sync.dma_start(wa_list[:], offs2)
         load_scales(was, wa_scales, WA_ROW)
-        load_words(waw, wa_words)
+        load_words(waw, wa_words, 0, WA_FIRST)
         load_scales(xs, x_scales, 0)
         nc.sync.dma_start(wb_list[:], offs3)
-        load_words(wbw, wb_words)
-        load_scales(wbs, wb_scales, WB_ROW)
+        load_scales(wbs, wb_scales, WB_ROW, range(1))
+        load_words(waw, wa_words, WA_FIRST, E * H)
+        load_words(wbw, wb_words, 0, E * N)
+        load_scales(wbs, wb_scales, WB_ROW, range(1, 4))
         nc.sync.dma_start(out=gate_sb[:], in_=gate)
         nc.sync.dma_start(out=ww[:].bitcast(I32), in_=w_words[0].bitcast(I32))
         load_scales(ws, w_scales, 0)
 
-        def first_layer(m):
-            slots = slice(P * m, P * m + P)
-            inner = slice(H * m, H * m + H)
-            h_ps = ps_h.tile([P, H], F32, name="h_ps")
+        sources = {
+            "xw": (xw[:].bitcast(U32), tok_list, P, U32),
+            "xs": (xs[:], tok_list, P, U8),
+            "waw": (waw[:].bitcast(U32), wa_list, H, U32),
+            "was": (was[:], wa_list, H, U8),
+            "wbw": (wbw[:].bitcast(U32), wb_list, N, U32),
+            "wbs": (wbs[:], wb_list, N, U8),
+        }
+        part = {}
+
+        def place(kind, tile, m0, m1, width):
+            for m in range(m0, m1):
+                part[kind, m] = (tile, width * (m - m0))
+
+        def view(kind, m, lo, hi, row=0):
+            tile, first = part[kind, m]
+            return tile[row:P, first + lo : first + hi]
+
+        def gather(kind, m0, m1, slot=None):
+            window, lst, width, dtype = sources[kind]
+            tile = sb("%s_g%d" % (kind, m0), width * (m1 - m0), dtype, slot)
+            nc.vector.tensor_copy(out=tile[:], in_=window.indirect(lst[:, width * m0 // 16 : width * m1 // 16]))
+            place(kind, tile, m0, m1, width)
+
+        def first_layer(m, slot):
+            h_ps = bank("h_ps%d" % m, slot)
             nc.tensor.matmul_mx(
                 out=h_ps[:],
-                lhsT=xw_g[:, slots].bitcast(FP8X4), lhsT_scale=xs_g[:, slots],
-                rhs=waw_g[:, inner].bitcast(FP8X4), rhs_scale=was_g[WA_ROW:P, inner],
+                lhsT=view("xw", m, 0, P).bitcast(FP8X4), lhsT_scale=view("xs", m, 0, P),
+                rhs=view("waw", m, 0, H).bitcast(FP8X4), rhs_scale=view("was", m, 0, H, WA_ROW),
                 start=True, stop=True,
             )
+            h_rows = sb("h_rows%d" % m, H, BF16)
             nc.scalar.activation(
-                out=h_rows[:, inner].rearrange("s (u p e) -> s u p e", u=2, e=2),
+                out=h_rows[:].rearrange("s (u p e) -> s u p e", u=2, e=2),
                 in_=h_ps[:].rearrange("s (p u e) -> s u p e", u=2, e=2),
                 func=GELU,
             )
-            pairs = h_rows[:, inner].bitcast(F32)
-            t_ps = ps_t.tile([P, 2, P], F32, name="t_ps")
+            place("h_rows", h_rows, m, m + 1, H)
+
+        def turn(m, slot):
+            t_ps = bank("t_ps%d" % m, slot)
+            pairs = view("h_rows", m, 0, H).bitcast(F32)
             for u in range(2):
-                nc.tensor.transpose(t_ps[:, u, :], pairs[:, P * u : P * u + P], ident[:])
+                nc.tensor.transpose(t_ps[:, P * u : P * u + P], pairs[:, P * u : P * u + P], ident[:])
             nc.scalar.copy(
-                out=h_cols[:, inner].bitcast(F32).rearrange("p (s u) -> p s u", u=2),
-                in_=t_ps[:].rearrange("p u s -> p s u"),
+                out=view("h_cols", m, 0, H).bitcast(F32).rearrange("p (s u) -> p s u", u=2),
+                in_=t_ps[:, 0 : 2 * P].rearrange("p (u s) -> p s u", u=2),
             )
 
-        def second_layer(m0, m1):
-            slots = slice(P * m0, P * m1)
-            nc.vector.quantize_mx(out=hq[:, slots].bitcast(FP8X4), scales=hs[:, slots], in_=h_cols[:, H * m0 : H * m1])
-            for c in range(2):
+        def quantize(m0, m1, slot=None):
+            hq = sb("hq%d" % m0, P * (m1 - m0), U32, slot)
+            hs = sb("hs%d" % m0, P * (m1 - m0), U8)
+            nc.vector.quantize_mx(out=hq[:].bitcast(FP8X4), scales=hs[:], in_=part["h_cols", m0][0][:])
+            place("hq", hq, m0, m1, P)
+            place("hs", hs, m0, m1, P)
+
+        def second_layer(halves, m0, m1, slot):
+            y_ps = bank("y_ps%d_%d" % (halves[0], m0), slot)
+            width = P * (m1 - m0)
+            for j, c in enumerate(halves):
                 for m in range(m0, m1):
-                    blk = slice(P * m, P * m + P)
-                    cols = slice(N * m + P * c, N * m + P * c + P)
+                    at = width * j + P * (m - m0)
                     nc.tensor.matmul_mx(
-                        out=y_ps[c][:, blk],
-                        lhsT=wbw_g[:, cols].bitcast(FP8X4), lhsT_scale=wbs_g[WB_ROW:P, cols],
-                        rhs=hq[:, blk].bitcast(FP8X4), rhs_scale=hs[:, blk],
+                        out=y_ps[:, at : at + P],
+                        lhsT=view("wbw", m, P * c, P * c + P).bitcast(FP8X4),
+                        lhsT_scale=view("wbs", m, P * c, P * c + P, WB_ROW),
+                        rhs=view("hq", m, 0, P).bitcast(FP8X4), rhs_scale=view("hs", m, 0, P),
                         start=True, stop=True,
                     )
-                nc.scalar.copy(out=y_sb[c][:, slots], in_=y_ps[c][:, slots])
+            return y_ps
 
-        def scatter(c, lo, hi):
+        def y_out(y_ps, lo, hi, name):
+            y_sb = sb(name, hi - lo, F32)
+            nc.scalar.copy(out=y_sb[:], in_=y_ps[:, lo:hi])
+            return y_sb
+
+        def scatter(c, m0, m1, values):
+            lo, hi = P * m0, P * m1
             nc.vector.tensor_tensor(
-                out=placed[c][:].indirect(tok_list[:, lo // 16 : hi // 16]),
-                in0=y_sb[c][:, lo:hi], in1=gate_sb[:, lo:hi], op=MULT,
+                out=placed[c][:].indirect(tok_list[:, lo // 16 : hi // 16]), in0=values, in1=gate_sb[:, lo:hi], op=MULT
             )
 
-        half = T // 2
-        for lo in (0, half):
-            gather(xw_g, xw[:].bitcast(U32), tok_list, lo, lo + half)
-        for lo in (0, 2 * H):
-            gather(was_g, was[:], wa_list, lo, lo + 2 * H)
-        gather(waw_g, waw[:].bitcast(U32), wa_list, 0, H)
-        for lo in (0, half):
-            gather(xs_g, xs[:], tok_list, lo, lo + half)
-        first_layer(0)
-        for m in range(1, B):
-            gather(waw_g, waw[:].bitcast(U32), wa_list, H * m, H * m + H)
-            first_layer(m)
-        for m0 in (0, 2):
-            gather(wbw_g, wbw[:].bitcast(U32), wb_list, N * m0, N * m0 + 2 * N)
-            gather(wbs_g, wbs[:], wb_list, N * m0, N * m0 + 2 * N)
-            second_layer(m0, m0 + 2)
-        for c in range(2):
+        def frozen(c, slot):
+            base_ps = bank("base_ps%d" % c, slot)
             nc.tensor.matmul_mx(
-                out=base_ps[c][:],
+                out=base_ps[:],
                 lhsT=ww[:, 2 * P * c : 2 * P * c + 2 * P].bitcast(FP4X4), lhsT_scale=ws[:, P * c : P * c + P],
                 rhs=xw[:].bitcast(FP8X4), rhs_scale=xs[:],
                 start=True, stop=True,
             )
-        for lo in (0, half):
-            for c in range(2):
-                scatter(c, lo, lo + half)
+            return base_ps
+
+        for m0, m1 in ((0, 1), (1, 2), (2, 4)):
+            place("h_cols", sb("h_cols%d" % m0, H * (m1 - m0), BF16), m0, m1, H)
+
+        gather("xw", 0, 2)
+        gather("xw", 2, 4)
+        gather("was", 0, 1)
+        gather("was", 1, 3)
+        gather("xs", 0, 2)
+        gather("waw", 0, 1)
+        first_layer(0, "a")
+        gather("waw", 1, 2)
+        first_layer(1, "b")
+        turn(0, "c")
+        turn(1, "d")
+        gather("waw", 2, 4)
+        gather("wbw", 0, 2, "waw_g0")
+        gather("wbs", 0, 2, "was_g0")
+        gather("xs", 2, 4, "h_rows0")
+        first_layer(2, "a")
+        gather("was", 3, 4, "h_rows1")
+        first_layer(3, "b")
+        quantize(0, 1)
+        y_ps = second_layer((0, 1), 0, 1, "e")
+        y00 = y_out(y_ps, 0, P, "y00")
+        y10 = y_out(y_ps, P, 2 * P, "y10")
+        quantize(1, 2)
+        gather("wbw", 2, 4, "h_cols0")
+        gather("wbs", 2, 4, "hs0")
+        turn(2, "c")
+        turn(3, "d")
+        scatter(0, 0, 1, y00[:])
+        scatter(1, 0, 1, y10[:])
+        quantize(2, 4, "y00")
+        y1 = y_out(second_layer((0, 1), 1, 2, "d"), 0, 2 * P, "y1")
+        y23 = [y_out(second_layer((c,), 2, 4, "fg"[c]), 0, 2 * P, "y23_%d" % c) for c in range(2)]
+        base = [frozen(c, "ed"[c]) for c in range(2)]
         for c in range(2):
-            nc.vector.tensor_tensor(out=res[c][:], in0=base_ps[c][:], in1=placed[c][:], op=ADD)
+            scatter(c, 1, 2, y1[:, P * c : P * c + P])
+        for c in range(2):
+            scatter(c, 2, 4, y23[c][:])
+        for c in range(2):
+            nc.vector.tensor_tensor(out=res[c][:], in0=base[c][:], in1=placed[c][:], op=ADD)
             nc.sync.dma_start(out=out[P * c : P * c + P, :], in_=res[c][:])

@@ -53,8 +53,8 @@ def tile_moe_dyl_gelu_kernel(
         def load_words(tile, words, lo, hi):
             nc.sync.dma_start(out=tile[:, lo:hi], in_=words[0, :, lo:hi, :].rearrange("p c d -> p (c d)").bitcast(I32))
 
-        def load_scales(tile, scales, row, rows=range(4)):
-            for r in rows:
+        def load_scales(tile, scales, row):
+            for r in range(4):
                 nc.sync.dma_start(out=tile[row + r : P : 32, :].bitcast(I32), in_=scales[0, r:16:4, :].bitcast(I32))
 
         for plane in (was, xs, wbs, ws):
@@ -69,10 +69,9 @@ def tile_moe_dyl_gelu_kernel(
         load_words(waw, wa_words, 0, WA_FIRST)
         load_scales(xs, x_scales, 0)
         nc.sync.dma_start(wb_list[:], offs3)
-        load_scales(wbs, wb_scales, WB_ROW, range(1))
         load_words(waw, wa_words, WA_FIRST, E * H)
         load_words(wbw, wb_words, 0, E * N)
-        load_scales(wbs, wb_scales, WB_ROW, range(1, 4))
+        load_scales(wbs, wb_scales, WB_ROW)
         nc.sync.dma_start(out=gate_sb[:], in_=gate)
         nc.sync.dma_start(out=ww[:].bitcast(I32), in_=w_words[0].bitcast(I32))
         load_scales(ws, w_scales, 0)
@@ -109,19 +108,19 @@ def tile_moe_dyl_gelu_kernel(
                 rhs=view("waw", m, 0, H).bitcast(FP8X4), rhs_scale=view("was", m, 0, H, WA_ROW),
                 start=True, stop=True,
             )
-            h_rows = sb("h_rows%d" % m, H, BF16)
-            nc.scalar.activation(
-                out=h_rows[:].rearrange("s (u p e) -> s u p e", u=2, e=2),
-                in_=h_ps[:].rearrange("s (p u e) -> s u p e", u=2, e=2),
-                func=GELU,
-            )
-            place("h_rows", h_rows, m, m + 1, H)
+            for u in range(2):
+                h_rows = sb("h_rows%d_%d" % (m, u), H // 2, BF16)
+                nc.scalar.activation(
+                    out=h_rows[:].rearrange("s (p e) -> s p e", e=2),
+                    in_=h_ps[:].rearrange("s (p u e) -> s u p e", u=2, e=2)[:, u],
+                    func=GELU,
+                )
+                part["h_rows", m, u] = h_rows
 
         def turn(m, slot):
             t_ps = bank("t_ps%d" % m, slot)
-            pairs = view("h_rows", m, 0, H).bitcast(F32)
             for u in range(2):
-                nc.tensor.transpose(t_ps[:, P * u : P * u + P], pairs[:, P * u : P * u + P], ident[:])
+                nc.tensor.transpose(t_ps[:, P * u : P * u + P], part["h_rows", m, u][:].bitcast(F32), ident[:])
             nc.scalar.copy(
                 out=view("h_cols", m, 0, H).bitcast(F32).rearrange("p (s u) -> p s u", u=2),
                 in_=t_ps[:, 0 : 2 * P].rearrange("p (u s) -> p s u", u=2),
@@ -175,8 +174,7 @@ def tile_moe_dyl_gelu_kernel(
 
         gather("xw", 0, 2)
         gather("xw", 2, 4)
-        gather("was", 0, 1)
-        gather("was", 1, 3)
+        gather("was", 0, 2)
         gather("xs", 0, 2)
         gather("waw", 0, 1)
         first_layer(0, "a")
@@ -185,12 +183,12 @@ def tile_moe_dyl_gelu_kernel(
         turn(0, "c")
         turn(1, "d")
         gather("waw", 2, 4)
-        gather("wbw", 0, 2, "waw_g0")
-        gather("wbs", 0, 2, "was_g0")
-        gather("xs", 2, 4, "h_rows0")
+        gather("was", 2, 4, "waw_g0")
+        gather("xs", 2, 4, "h_rows0_1")
         first_layer(2, "a")
-        gather("was", 3, 4, "h_rows1")
         first_layer(3, "b")
+        gather("wbw", 0, 2, "h_rows1_0")
+        gather("wbs", 0, 2, "h_rows1_1")
         quantize(0, 1)
         y_ps = second_layer((0, 1), 0, 1, "e")
         y00 = y_out(y_ps, 0, P, "y00")

@@ -22,6 +22,7 @@ ADD = mybir.AluOpType.add
 WA_ROW = 4
 WB_ROW = 8
 WA_FIRST = 1920
+SPLIT = 320
 
 
 def tile_moe_dyl_gelu_kernel(
@@ -202,12 +203,20 @@ def tile_moe_dyl_gelu_kernel(
         scatter(1, 0, 1, y10[:])
         quantize(2, 4, "y00")
         y1 = y_out(second_layer((0, 1), 1, 2, "d"), 0, 2 * P, "y1")
-        y23 = [y_out(second_layer((c,), 2, 4, "fg"[c]), 0, 2 * P, "y23_%d" % c) for c in range(2)]
+        y023 = y_out(second_layer((0,), 2, 4, "f"), 0, 2 * P, "y023")
+        y123_ps = second_layer((1,), 2, 4, "g")
         base = [frozen(c, "ed"[c]) for c in range(2)]
+        base0 = y_out(base[0], 0, SPLIT, "base0")
         for c in range(2):
             scatter(c, 1, 2, y1[:, P * c : P * c + P])
-        for c in range(2):
-            scatter(c, 2, 4, y23[c][:])
-        for c in range(2):
-            nc.vector.tensor_tensor(out=res[c][:], in0=base[c][:], in1=placed[c][:], op=ADD)
-            nc.sync.dma_start(out=out[P * c : P * c + P, :], in_=res[c][:])
+        res0b = sb("res0b", T - SPLIT, F32)
+        gated = sb("gated", 2 * P, F32)
+        nc.vector.tensor_tensor(out=gated[:], in0=y123_ps[:, 0 : 2 * P], in1=gate_sb[:, 2 * P : T], op=MULT)
+        scatter(0, 2, 4, y023[:])
+        nc.vector.tensor_copy(out=placed[1][:].indirect(tok_list[:, 2 * P // 16 : T // 16]), in_=gated[:])
+        nc.gpsimd.tensor_tensor(out=res[0][:, 0:SPLIT], in0=base0[:, 0:SPLIT], in1=placed[0][:, 0:SPLIT], op=ADD)
+        nc.vector.tensor_tensor(out=res0b[:], in0=base[0][:, SPLIT:T], in1=placed[0][:, SPLIT:T], op=ADD)
+        nc.sync.dma_start(out=out[0:P, 0:SPLIT], in_=res[0][:, 0:SPLIT])
+        nc.sync.dma_start(out=out[0:P, SPLIT:T], in_=res0b[:])
+        nc.vector.tensor_tensor(out=res[1][:], in0=base[1][:], in1=placed[1][:], op=ADD)
+        nc.sync.dma_start(out=out[P : 2 * P, :], in_=res[1][:])

@@ -16,13 +16,15 @@ U8 = mybir.dt.uint8
 FP8X4 = mybir.dt.float8_e4m3fn_x4
 FP4X4 = mybir.dt.float4_e2m1fn_x4
 GELU = mybir.ActivationFunctionType.Gelu_apprx_tanh
+COPY = mybir.ActivationFunctionType.Copy
 MULT = mybir.AluOpType.mult
 ADD = mybir.AluOpType.add
 
 WA_ROW = 4
 WB_ROW = 8
-WA_FIRST = 1920
-SPLIT = 320
+WA_FIRST = 1280
+TOKEN_WINDOW = 704
+SPLIT = 256
 
 
 def tile_moe_dyl_gelu_kernel(
@@ -42,24 +44,27 @@ def tile_moe_dyl_gelu_kernel(
         tok_list = sb("tok_list", T // 16, U16)
         wa_list = sb("wa_list", B * H // 16, U16)
         wb_list = sb("wb_list", B * N // 16, U16)
-        xw, xs = sb("xw", T, I32), sb("xs", T, U8)
+        xw, xs = sb("xw", TOKEN_WINDOW, I32), sb("xs", TOKEN_WINDOW, U8)
         waw, was = sb("waw", E * H, I32), sb("was", E * H, U8)
         wbw, wbs = sb("wbw", E * N, I32), sb("wbs", E * N, U8)
         ww, ws = sb("ww", 2 * N, U8), sb("ws", N, U8)
         gate_sb = sb("gate_sb", T, F32)
+        gate_col = sb("gate_col", 2, F32)
         ident = sb("ident", P, F32)
         placed = [sb("placed%d" % c, T, F32) for c in range(2)]
-        res = [sb("res%d" % c, T, F32) for c in range(2)]
 
         def load_words(tile, words, lo, hi):
             nc.sync.dma_start(out=tile[:, lo:hi], in_=words[0, :, lo:hi, :].rearrange("p c d -> p (c d)").bitcast(I32))
 
         def load_scales(tile, scales, row):
             for r in range(4):
-                nc.sync.dma_start(out=tile[row + r : P : 32, :].bitcast(I32), in_=scales[0, r:16:4, :].bitcast(I32))
+                nc.sync.dma_start(
+                    out=tile[row + r : P : 32, 0 : scales.shape[2]].bitcast(I32), in_=scales[0, r:16:4, :].bitcast(I32)
+                )
 
         for plane in (was, xs, wbs, ws):
             nc.vector.memset(plane[:].bitcast(I32), 0)
+        nc.vector.memset(xw[:, T:TOKEN_WINDOW], 0)
         nc.vector.memset(ident[:], 0.0)
 
         make_identity(nc, ident[:], nomemset=True)
@@ -76,6 +81,8 @@ def tile_moe_dyl_gelu_kernel(
         nc.sync.dma_start(out=gate_sb[:], in_=gate)
         nc.sync.dma_start(out=ww[:].bitcast(I32), in_=w_words[0].bitcast(I32))
         load_scales(ws, w_scales, 0)
+        with nc.allow_non_contiguous_dma(reason="one gate value a partition"):
+            nc.sync.dma_start(out=gate_col[:], in_=gate[0:1, 0 : 2 * P].rearrange("o (m p) -> p (o m)", p=P))
 
         sources = {
             "xw": (xw[:].bitcast(U32), tok_list, P, U32),
@@ -160,63 +167,78 @@ def tile_moe_dyl_gelu_kernel(
                 out=placed[c][:].indirect(tok_list[:, lo // 16 : hi // 16]), in0=values, in1=gate_sb[:, lo:hi], op=MULT
             )
 
-        def frozen(c, slot):
-            base_ps = bank("base_ps%d" % c, slot)
+        def frozen(c, lo, hi, slot):
+            base_ps = bank("base_ps%d_%d" % (c, lo), slot)
             nc.tensor.matmul_mx(
-                out=base_ps[:],
+                out=base_ps[:, 0 : hi - lo],
                 lhsT=ww[:, 2 * P * c : 2 * P * c + 2 * P].bitcast(FP4X4), lhsT_scale=ws[:, P * c : P * c + P],
-                rhs=xw[:].bitcast(FP8X4), rhs_scale=xs[:],
+                rhs=xw[:, lo:hi].bitcast(FP8X4), rhs_scale=xs[:, lo:hi],
                 start=True, stop=True,
             )
             return base_ps
 
-        for m0, m1 in ((0, 1), (1, 2), (2, 4)):
+        def gated_turned(c, m0, m1, slot, back_slot):
+            yt_ps = bank("yt_ps", slot)
+            for m in range(m0, m1):
+                nc.tensor.matmul_mx(
+                    out=yt_ps[:, P * m : P * m + P],
+                    lhsT=view("hq", m, 0, P).bitcast(FP8X4), lhsT_scale=view("hs", m, 0, P),
+                    rhs=view("wbw", m, P * c, P * c + P).bitcast(FP8X4),
+                    rhs_scale=view("wbs", m, P * c, P * c + P, WB_ROW),
+                    start=True, stop=True,
+                )
+            yt = sb("yt", P * (m1 - m0), F32)
+            for m in range(m0, m1):
+                nc.scalar.activation(
+                    out=yt[:, P * m : P * m + P], in_=yt_ps[:, P * m : P * m + P], func=COPY, scale=gate_col[:, m : m + 1]
+                )
+            back_ps = bank("back_ps", back_slot)
+            for m in range(m0, m1):
+                nc.tensor.transpose(back_ps[:, P * m : P * m + P], yt[:, P * m : P * m + P], ident[:])
+            return y_out(back_ps, 0, P * (m1 - m0), "gated")
+
+        for m0, m1 in ((0, 2), (2, 4)):
             place("h_cols", sb("h_cols%d" % m0, H * (m1 - m0), BF16), m0, m1, H)
 
-        gather("xw", 0, 2)
-        gather("xw", 2, 4)
+        gather("xw", 0, 4)
         gather("was", 0, 2)
-        gather("xs", 0, 2)
+        gather("xs", 0, 4)
         gather("waw", 0, 1)
         first_layer(0, "a")
         gather("waw", 1, 2)
         first_layer(1, "b")
         turn(0, "c")
         turn(1, "d")
-        gather("waw", 2, 4)
+        gather("waw", 2, 3)
         gather("was", 2, 4, "waw_g0")
-        gather("xs", 2, 4, "h_rows0_1")
-        first_layer(2, "a")
-        first_layer(3, "b")
-        gather("wbw", 0, 2, "h_rows1_0")
-        gather("wbs", 0, 2, "h_rows1_1")
-        quantize(0, 1)
-        y_ps = second_layer((0, 1), 0, 1, "e")
-        y00 = y_out(y_ps, 0, P, "y00")
-        y10 = y_out(y_ps, P, 2 * P, "y10")
-        quantize(1, 2)
-        gather("wbw", 2, 4, "h_cols0")
-        gather("wbs", 2, 4, "hs0")
-        turn(2, "c")
+        gather("waw", 3, 4, "waw_g1")
+        first_layer(2, "b")
+        first_layer(3, "c")
+        gather("wbw", 0, 2, "was_g0")
+        gather("wbs", 0, 2, "h_rows0_1")
+        quantize(0, 2)
+        gather("wbw", 2, 4, "waw_g1")
+        gather("wbs", 2, 4, "waw_g0")
+        turn(2, "a")
         turn(3, "d")
-        scatter(0, 0, 1, y00[:])
-        scatter(1, 0, 1, y10[:])
-        quantize(2, 4, "y00")
-        y1 = y_out(second_layer((0, 1), 1, 2, "d"), 0, 2 * P, "y1")
-        y023 = y_out(second_layer((0,), 2, 4, "f"), 0, 2 * P, "y023")
-        y123_ps = second_layer((1,), 2, 4, "g")
-        base = [frozen(c, "ed"[c]) for c in range(2)]
-        base0 = y_out(base[0], 0, SPLIT, "base0")
-        for c in range(2):
-            scatter(c, 1, 2, y1[:, P * c : P * c + P])
-        res0b = sb("res0b", T - SPLIT, F32)
-        gated = sb("gated", 2 * P, F32)
-        nc.vector.tensor_tensor(out=gated[:], in0=y123_ps[:, 0 : 2 * P], in1=gate_sb[:, 2 * P : T], op=MULT)
+        y001 = y_out(second_layer((0,), 0, 2, "c"), 0, 2 * P, "y001")
+        quantize(2, 4)
+        y123 = y_out(second_layer((1,), 2, 4, "a"), 0, 2 * P, "y123")
+        y023 = y_out(second_layer((0,), 2, 4, "b"), 0, 2 * P, "y023")
+        gated = gated_turned(1, 0, 2, "a", "d")
+        base0 = y_out(frozen(0, 0, SPLIT, "b"), 0, SPLIT, "base0")
+        base1_ps = frozen(1, 0, T, "a")
+        base0_ps = frozen(0, SPLIT, T, "d")
+        scatter(0, 0, 2, y001[:])
+        scatter(1, 2, 4, y123[:])
         scatter(0, 2, 4, y023[:])
-        nc.vector.tensor_copy(out=placed[1][:].indirect(tok_list[:, 2 * P // 16 : T // 16]), in_=gated[:])
-        nc.gpsimd.tensor_tensor(out=res[0][:, 0:SPLIT], in0=base0[:, 0:SPLIT], in1=placed[0][:, 0:SPLIT], op=ADD)
-        nc.vector.tensor_tensor(out=res0b[:], in0=base[0][:, SPLIT:T], in1=placed[0][:, SPLIT:T], op=ADD)
-        nc.sync.dma_start(out=out[0:P, 0:SPLIT], in_=res[0][:, 0:SPLIT])
+        nc.vector.tensor_copy(out=placed[1][:].indirect(tok_list[:, 0 : 2 * P // 16]), in_=gated[:])
+        res0a = sb("res0a", SPLIT, F32)
+        res0b = sb("res0b", T - SPLIT, F32)
+        res1 = sb("res1", T, F32)
+        nc.gpsimd.tensor_tensor(out=res0a[:], in0=base0[:], in1=placed[0][:, 0:SPLIT], op=ADD)
+        nc.vector.tensor_tensor(out=res0b[:], in0=base0_ps[:, 0 : T - SPLIT], in1=placed[0][:, SPLIT:T], op=ADD)
+        nc.sync.dma_start(out=out[0:P, 0:SPLIT], in_=res0a[:])
         nc.sync.dma_start(out=out[0:P, SPLIT:T], in_=res0b[:])
-        nc.vector.tensor_tensor(out=res[1][:], in0=base[1][:], in1=placed[1][:], op=ADD)
-        nc.sync.dma_start(out=out[P : 2 * P, :], in_=res[1][:])
+        nc.vector.tensor_tensor(out=res1[:], in0=base1_ps[:], in1=placed[1][:], op=ADD)
+        nc.sync.dma_start(out=out[P : 2 * P, :], in_=res1[:])

@@ -53,8 +53,8 @@ def tile_moe_dyl_gelu_kernel(
         ident = sb("ident", P, F32)
         placed = [sb("placed%d" % c, T, F32) for c in range(2)]
 
-        def load_words(tile, words, lo, hi):
-            nc.sync.dma_start(out=tile[:, lo:hi], in_=words[0, :, lo:hi, :].rearrange("p c d -> p (c d)").bitcast(I32))
+        def load_words(tile, words, lo, hi, queue=nc.sync):
+            queue.dma_start(out=tile[:, lo:hi], in_=words[0, :, lo:hi, :].rearrange("p c d -> p (c d)").bitcast(I32))
 
         def load_scales(tile, scales, row):
             for r in range(4):
@@ -68,7 +68,7 @@ def tile_moe_dyl_gelu_kernel(
         nc.vector.memset(ident[:], 0.0)
 
         make_identity(nc, ident[:], nomemset=True)
-        load_words(xw, x_words, 0, T)
+        load_words(xw, x_words, 0, T, nc.scalar)
         nc.sync.dma_start(tok_list[:], offs)
         nc.sync.dma_start(wa_list[:], offs2)
         load_scales(was, wa_scales, WA_ROW)

@@ -24,7 +24,8 @@ WA_ROW = 4
 WB_ROW = 8
 WA_FIRST = 1280
 TOKEN_WINDOW = 704
-SPLIT = 256
+SPLIT = 384
+TURNED = 3
 
 
 def tile_moe_dyl_gelu_kernel(
@@ -49,7 +50,7 @@ def tile_moe_dyl_gelu_kernel(
         wbw, wbs = sb("wbw", E * N, I32), sb("wbs", E * N, U8)
         ww, ws = sb("ww", 2 * N, U8), sb("ws", N, U8)
         gate_sb = sb("gate_sb", T, F32)
-        gate_col = sb("gate_col", 2, F32)
+        gate_col = sb("gate_col", TURNED, F32)
         ident = sb("ident", P, F32)
         placed = [sb("placed%d" % c, T, F32) for c in range(2)]
 
@@ -78,11 +79,11 @@ def tile_moe_dyl_gelu_kernel(
         load_words(waw, wa_words, WA_FIRST, E * H)
         load_words(wbw, wb_words, 0, E * N)
         load_scales(wbs, wb_scales, WB_ROW)
+        with nc.allow_non_contiguous_dma(reason="one gate value a partition"):
+            nc.sync.dma_start(out=gate_col[:], in_=gate[0:1, 0 : TURNED * P].rearrange("o (m p) -> p (o m)", p=P))
         nc.sync.dma_start(out=gate_sb[:], in_=gate)
         nc.sync.dma_start(out=ww[:].bitcast(I32), in_=w_words[0].bitcast(I32))
         load_scales(ws, w_scales, 0)
-        with nc.allow_non_contiguous_dma(reason="one gate value a partition"):
-            nc.sync.dma_start(out=gate_col[:], in_=gate[0:1, 0 : 2 * P].rearrange("o (m p) -> p (o m)", p=P))
 
         sources = {
             "xw": (xw[:].bitcast(U32), tok_list, P, U32),
@@ -167,18 +168,17 @@ def tile_moe_dyl_gelu_kernel(
                 out=placed[c][:].indirect(tok_list[:, lo // 16 : hi // 16]), in0=values, in1=gate_sb[:, lo:hi], op=MULT
             )
 
-        def frozen(c, lo, hi, slot):
-            base_ps = bank("base_ps%d_%d" % (c, lo), slot)
+        def frozen(c, lo, hi, base_ps):
             nc.tensor.matmul_mx(
-                out=base_ps[:, 0 : hi - lo],
+                out=base_ps[:, lo:hi],
                 lhsT=ww[:, 2 * P * c : 2 * P * c + 2 * P].bitcast(FP4X4), lhsT_scale=ws[:, P * c : P * c + P],
                 rhs=xw[:, lo:hi].bitcast(FP8X4), rhs_scale=xs[:, lo:hi],
                 start=True, stop=True,
             )
             return base_ps
 
-        def gated_turned(c, m0, m1, slot, back_slot):
-            yt_ps = bank("yt_ps", slot)
+        def gated_rows(c, m0, m1, slot, yt):
+            yt_ps = bank("yt_ps%d" % m0, slot)
             for m in range(m0, m1):
                 nc.tensor.matmul_mx(
                     out=yt_ps[:, P * m : P * m + P],
@@ -187,15 +187,10 @@ def tile_moe_dyl_gelu_kernel(
                     rhs_scale=view("wbs", m, P * c, P * c + P, WB_ROW),
                     start=True, stop=True,
                 )
-            yt = sb("yt", P * (m1 - m0), F32)
             for m in range(m0, m1):
                 nc.scalar.activation(
                     out=yt[:, P * m : P * m + P], in_=yt_ps[:, P * m : P * m + P], func=COPY, scale=gate_col[:, m : m + 1]
                 )
-            back_ps = bank("back_ps", back_slot)
-            for m in range(m0, m1):
-                nc.tensor.transpose(back_ps[:, P * m : P * m + P], yt[:, P * m : P * m + P], ident[:])
-            return y_out(back_ps, 0, P * (m1 - m0), "gated")
 
         for m0, m1 in ((0, 2), (2, 4)):
             place("h_cols", sb("h_cols%d" % m0, H * (m1 - m0), BF16), m0, m1, H)
@@ -223,22 +218,32 @@ def tile_moe_dyl_gelu_kernel(
         turn(3, "d")
         y001 = y_out(second_layer((0,), 0, 2, "c"), 0, 2 * P, "y001")
         quantize(2, 4)
-        y123 = y_out(second_layer((1,), 2, 4, "a"), 0, 2 * P, "y123")
+        yt = sb("yt", TURNED * P, F32)
+        gated_rows(1, 0, 2, "d", yt)
+        y13 = y_out(second_layer((1,), 3, 4, "a"), 0, P, "y13")
         y023 = y_out(second_layer((0,), 2, 4, "b"), 0, 2 * P, "y023")
-        gated = gated_turned(1, 0, 2, "a", "d")
-        base0 = y_out(frozen(0, 0, SPLIT, "b"), 0, SPLIT, "base0")
-        base1_ps = frozen(1, 0, T, "a")
-        base0_ps = frozen(0, SPLIT, T, "d")
+        gated_rows(1, 2, 3, "c", yt)
+        back_ps = bank("back_ps", "b")
+        for m in range(TURNED):
+            nc.tensor.transpose(back_ps[:, P * m : P * m + P], yt[:, P * m : P * m + P], ident[:])
+        gated = y_out(back_ps, 0, TURNED * P, "gated")
+        early_ps = bank("base0_early", "c")
+        frozen(0, 0, 2 * P, early_ps)
+        base0 = y_out(frozen(0, 2 * P, SPLIT, early_ps), 0, SPLIT, "base0")
+        base0_ps = frozen(0, SPLIT, T, bank("base0_late", "b"))
+        base1_ps = frozen(1, 0, T, bank("base1", "c"))
         scatter(0, 0, 2, y001[:])
-        scatter(1, 2, 4, y123[:])
+        scatter(1, 3, 4, y13[:])
         scatter(0, 2, 4, y023[:])
-        nc.vector.tensor_copy(out=placed[1][:].indirect(tok_list[:, 0 : 2 * P // 16]), in_=gated[:])
+        nc.vector.tensor_copy(out=placed[1][:].indirect(tok_list[:, 0 : TURNED * P // 16]), in_=gated[:])
         res0a = sb("res0a", SPLIT, F32)
         res0b = sb("res0b", T - SPLIT, F32)
         res1 = sb("res1", T, F32)
         nc.gpsimd.tensor_tensor(out=res0a[:], in0=base0[:], in1=placed[0][:, 0:SPLIT], op=ADD)
-        nc.vector.tensor_tensor(out=res0b[:], in0=base0_ps[:, 0 : T - SPLIT], in1=placed[0][:, SPLIT:T], op=ADD)
-        nc.sync.dma_start(out=out[0:P, 0:SPLIT], in_=res0a[:])
+        nc.scalar.dma_start(out=out[0:P, 0:SPLIT], in_=res0a[:])
+        nc.vector.tensor_tensor(out=res0b[:], in0=base0_ps[:, SPLIT:T], in1=placed[0][:, SPLIT:T], op=ADD)
         nc.sync.dma_start(out=out[0:P, SPLIT:T], in_=res0b[:])
-        nc.vector.tensor_tensor(out=res1[:], in0=base1_ps[:], in1=placed[1][:], op=ADD)
-        nc.sync.dma_start(out=out[P : 2 * P, :], in_=res1[:])
+        for lo in (0, T // 2):
+            hi = lo + T // 2
+            nc.vector.tensor_tensor(out=res1[:, lo:hi], in0=base1_ps[:, lo:hi], in1=placed[1][:, lo:hi], op=ADD)
+            nc.sync.dma_start(out=out[P : 2 * P, lo:hi], in_=res1[:, lo:hi])

@@ -1,7 +1,6 @@
 from contextlib import ExitStack
 
 import concourse.mybir as mybir
-from concourse.masks import make_identity
 
 K, T, E, B, H, N = 512, 512, 4, 4, 512, 256
 P = 128
@@ -22,10 +21,8 @@ ADD = mybir.AluOpType.add
 
 WA_ROW = 4
 WB_ROW = 8
-WA_FIRST = 1280
 TOKEN_WINDOW = 704
-SPLIT = 384
-TURNED = 3
+WA_FIRST = 1280
 
 
 def tile_moe_dyl_gelu_kernel(
@@ -34,9 +31,12 @@ def tile_moe_dyl_gelu_kernel(
     nc = tc.nc
     with ExitStack() as ctx:
         keep = ctx.enter_context(tc.tile_pool(name="keep", bufs=1))
+        shared = ctx.enter_context(tc.tile_pool(name="shared", bufs=1))
         psum = ctx.enter_context(tc.psum_pool(name="psum", bufs=1))
 
         def sb(name, cols, dtype, slot=None):
+            if isinstance(slot, int):
+                return shared.tile([P, cols], dtype, name=name, align_bytes=64, offset=slot)
             return keep.tile([P, cols], dtype, name=name, tag=slot or name, align_bytes=64)
 
         def bank(name, slot):
@@ -50,37 +50,31 @@ def tile_moe_dyl_gelu_kernel(
         wbw, wbs = sb("wbw", E * N, I32), sb("wbs", E * N, U8)
         ww, ws = sb("ww", 2 * N, U8), sb("ws", N, U8)
         gate_sb = sb("gate_sb", T, F32)
-        gate_col = sb("gate_col", TURNED, F32)
-        ident = sb("ident", P, F32)
         placed = [sb("placed%d" % c, T, F32) for c in range(2)]
 
         def load_words(tile, words, lo, hi, queue=nc.sync):
             queue.dma_start(out=tile[:, lo:hi], in_=words[0, :, lo:hi, :].rearrange("p c d -> p (c d)").bitcast(I32))
 
-        def load_scales(tile, scales, row):
+        def load_scales(tile, scales, row, queue=nc.sync):
             for r in range(4):
-                nc.sync.dma_start(
+                queue.dma_start(
                     out=tile[row + r : P : 32, 0 : scales.shape[2]].bitcast(I32), in_=scales[0, r:16:4, :].bitcast(I32)
                 )
 
         for plane in (was, xs, wbs, ws):
             nc.vector.memset(plane[:].bitcast(I32), 0)
         nc.vector.memset(xw[:, T:TOKEN_WINDOW], 0)
-        nc.vector.memset(ident[:], 0.0)
 
-        make_identity(nc, ident[:], nomemset=True)
         load_words(xw, x_words, 0, T, nc.scalar)
         nc.sync.dma_start(tok_list[:], offs)
         nc.sync.dma_start(wa_list[:], offs2)
         load_scales(was, wa_scales, WA_ROW)
         load_words(waw, wa_words, 0, WA_FIRST)
         load_scales(xs, x_scales, 0)
-        nc.sync.dma_start(wb_list[:], offs3)
         load_words(waw, wa_words, WA_FIRST, E * H)
+        nc.sync.dma_start(wb_list[:], offs3)
         load_words(wbw, wb_words, 0, E * N)
         load_scales(wbs, wb_scales, WB_ROW)
-        with nc.allow_non_contiguous_dma(reason="one gate value a partition"):
-            nc.sync.dma_start(out=gate_col[:], in_=gate[0:1, 0 : TURNED * P].rearrange("o (m p) -> p (o m)", p=P))
         nc.sync.dma_start(out=gate_sb[:], in_=gate)
         nc.sync.dma_start(out=ww[:].bitcast(I32), in_=w_words[0].bitcast(I32))
         load_scales(ws, w_scales, 0)
@@ -95,10 +89,6 @@ def tile_moe_dyl_gelu_kernel(
         }
         part = {}
 
-        def place(kind, tile, m0, m1, width):
-            for m in range(m0, m1):
-                part[kind, m] = (tile, width * (m - m0))
-
         def view(kind, m, lo, hi, row=0):
             tile, first = part[kind, m]
             return tile[row:P, first + lo : first + hi]
@@ -106,48 +96,46 @@ def tile_moe_dyl_gelu_kernel(
         def gather(kind, m0, m1, slot=None):
             window, lst, width, dtype = sources[kind]
             tile = sb("%s_g%d" % (kind, m0), width * (m1 - m0), dtype, slot)
-            nc.vector.tensor_copy(out=tile[:], in_=window.indirect(lst[:, width * m0 // 16 : width * m1 // 16]))
-            place(kind, tile, m0, m1, width)
+            target = tile[:]
+            if lst is wa_list:
+                target = target.rearrange("p (m t q) -> p m q t", t=4, q=P)
+            nc.vector.tensor_copy(out=target, in_=window.indirect(lst[:, width * m0 // 16 : width * m1 // 16]))
+            for m in range(m0, m1):
+                part[kind, m] = (tile, width * (m - m0))
 
         def first_layer(m, slot):
             h_ps = bank("h_ps%d" % m, slot)
-            nc.tensor.matmul_mx(
-                out=h_ps[:],
-                lhsT=view("xw", m, 0, P).bitcast(FP8X4), lhsT_scale=view("xs", m, 0, P),
-                rhs=view("waw", m, 0, H).bitcast(FP8X4), rhs_scale=view("was", m, 0, H, WA_ROW),
-                start=True, stop=True,
-            )
-            for u in range(2):
-                h_rows = sb("h_rows%d_%d" % (m, u), H // 2, BF16)
-                nc.scalar.activation(
-                    out=h_rows[:].rearrange("s (p e) -> s p e", e=2),
-                    in_=h_ps[:].rearrange("s (p u e) -> s u p e", u=2, e=2)[:, u],
-                    func=GELU,
+            for t in range(4):
+                nc.tensor.matmul_mx(
+                    out=h_ps[:, P * t : P * t + P],
+                    lhsT=view("waw", m, P * t, P * t + P).bitcast(FP8X4),
+                    lhsT_scale=view("was", m, P * t, P * t + P, WA_ROW),
+                    rhs=view("xw", m, 0, P).bitcast(FP8X4), rhs_scale=view("xs", m, 0, P),
+                    start=True, stop=True,
                 )
-                part["h_rows", m, u] = h_rows
-
-        def turn(m, slot):
-            t_ps = bank("t_ps%d" % m, slot)
-            for u in range(2):
-                nc.tensor.transpose(t_ps[:, P * u : P * u + P], part["h_rows", m, u][:].bitcast(F32), ident[:])
-            nc.scalar.copy(
-                out=view("h_cols", m, 0, H).bitcast(F32).rearrange("p (s u) -> p s u", u=2),
-                in_=t_ps[:, 0 : 2 * P].rearrange("p (u s) -> p s u", u=2),
+            nc.scalar.activation(
+                out=view("h", m, 0, H).rearrange("p (s t) -> p s t", t=4),
+                in_=h_ps[:].rearrange("p (t s) -> p s t", t=4),
+                func=GELU,
             )
 
-        def quantize(m0, m1, slot=None):
-            hq = sb("hq%d" % m0, P * (m1 - m0), U32, slot)
-            hs = sb("hs%d" % m0, P * (m1 - m0), U8)
-            nc.vector.quantize_mx(out=hq[:].bitcast(FP8X4), scales=hs[:], in_=part["h_cols", m0][0][:])
-            place("hq", hq, m0, m1, P)
-            place("hs", hs, m0, m1, P)
+        def new(kind, m0, m1, width, dtype, slot=None):
+            tile = sb("%s%d" % (kind, m0), width * (m1 - m0), dtype, slot)
+            for m in range(m0, m1):
+                part[kind, m] = (tile, width * (m - m0))
+            return tile
 
-        def second_layer(halves, m0, m1, slot):
-            y_ps = bank("y_ps%d_%d" % (halves[0], m0), slot)
+        def quantize(m0, m1, hq_slot=None):
+            hq = new("hq", m0, m1, P, U32, hq_slot)
+            hs = new("hs", m0, m1, P, U8)
+            nc.vector.quantize_mx(out=hq[:].bitcast(FP8X4), scales=hs[:], in_=view("h", m0, 0, H * (m1 - m0)))
+
+        def second_layer(m0, m1, slot):
+            y_ps = bank("y_ps%d" % m0, slot)
             width = P * (m1 - m0)
-            for j, c in enumerate(halves):
-                for m in range(m0, m1):
-                    at = width * j + P * (m - m0)
+            for m in range(m0, m1):
+                for c in range(2):
+                    at = width * c + P * (m - m0)
                     nc.tensor.matmul_mx(
                         out=y_ps[:, at : at + P],
                         lhsT=view("wbw", m, P * c, P * c + P).bitcast(FP8X4),
@@ -155,95 +143,82 @@ def tile_moe_dyl_gelu_kernel(
                         rhs=view("hq", m, 0, P).bitcast(FP8X4), rhs_scale=view("hs", m, 0, P),
                         start=True, stop=True,
                     )
-            return y_ps
+            part["y", m0] = y_ps
 
-        def y_out(y_ps, lo, hi, name):
-            y_sb = sb(name, hi - lo, F32)
-            nc.scalar.copy(out=y_sb[:], in_=y_ps[:, lo:hi])
-            return y_sb
-
-        def scatter(c, m0, m1, values):
-            lo, hi = P * m0, P * m1
+        def gated(m0, m1):
+            width = P * (m1 - m0)
+            gy = sb("gy%d" % m0, 2 * width, F32)
             nc.vector.tensor_tensor(
-                out=placed[c][:].indirect(tok_list[:, lo // 16 : hi // 16]), in0=values, in1=gate_sb[:, lo:hi], op=MULT
+                out=gy[:].rearrange("p (c s) -> p c s", c=2),
+                in0=part["y", m0][:, 0 : 2 * width].rearrange("p (c s) -> p c s", c=2),
+                in1=gate_sb[:, P * m0 : P * m1].unsqueeze(1).to_broadcast([P, 2, width]),
+                op=MULT,
             )
+            for m in range(m0, m1):
+                for c in range(2):
+                    part[("gy", c), m] = (gy, width * c + P * (m - m0))
 
-        def frozen(c, lo, hi, base_ps):
+        def scatter(m0, m1, c, on_vector=False):
+            target = placed[c][:].indirect(tok_list[:, P * m0 // 16 : P * m1 // 16])
+            values = view(("gy", c), m0, 0, P * (m1 - m0))
+            if on_vector:
+                nc.vector.tensor_copy(out=target, in_=values)
+            else:
+                nc.scalar.activation(out=target, in_=values, func=COPY)
+
+        def frozen(c):
+            base_ps = bank("base%d" % c, "base%d" % c)
             nc.tensor.matmul_mx(
-                out=base_ps[:, lo:hi],
+                out=base_ps[:],
                 lhsT=ww[:, 2 * P * c : 2 * P * c + 2 * P].bitcast(FP4X4), lhsT_scale=ws[:, P * c : P * c + P],
-                rhs=xw[:, lo:hi].bitcast(FP8X4), rhs_scale=xs[:, lo:hi],
+                rhs=xw[:, 0:T].bitcast(FP8X4), rhs_scale=xs[:, 0:T],
                 start=True, stop=True,
             )
             return base_ps
 
-        def gated_rows(c, m0, m1, slot, yt):
-            yt_ps = bank("yt_ps%d" % m0, slot)
-            for m in range(m0, m1):
-                nc.tensor.matmul_mx(
-                    out=yt_ps[:, P * m : P * m + P],
-                    lhsT=view("hq", m, 0, P).bitcast(FP8X4), lhsT_scale=view("hs", m, 0, P),
-                    rhs=view("wbw", m, P * c, P * c + P).bitcast(FP8X4),
-                    rhs_scale=view("wbs", m, P * c, P * c + P, WB_ROW),
-                    start=True, stop=True,
-                )
-            for m in range(m0, m1):
-                nc.scalar.activation(
-                    out=yt[:, P * m : P * m + P], in_=yt_ps[:, P * m : P * m + P], func=COPY, scale=gate_col[:, m : m + 1]
-                )
+        def finish(c, lo, hi, base_ps, queue):
+            res = sb("res%d_%d" % (c, lo), hi - lo, F32)
+            nc.vector.tensor_tensor(out=res[:], in0=base_ps[:, lo:hi], in1=placed[c][:, lo:hi], op=ADD)
+            queue.dma_start(out=out[P * c : P * c + P, lo:hi], in_=res[:])
 
-        for m0, m1 in ((0, 2), (2, 4)):
-            place("h_cols", sb("h_cols%d" % m0, H * (m1 - m0), BF16), m0, m1, H)
-
+        new("h", 0, 2, H, BF16, 0)
+        new("h", 2, 3, H, BF16)
+        new("h", 3, 4, H, BF16)
         gather("xw", 0, 4)
         gather("was", 0, 2)
-        gather("xs", 0, 4)
+        gather("xs", 0, 2)
         gather("waw", 0, 1)
         first_layer(0, "a")
         gather("waw", 1, 2)
         first_layer(1, "b")
-        turn(0, "c")
-        turn(1, "d")
-        gather("waw", 2, 3)
-        gather("was", 2, 4, "waw_g0")
-        gather("waw", 3, 4, "waw_g1")
-        first_layer(2, "b")
-        first_layer(3, "c")
-        gather("wbw", 0, 2, "was_g0")
-        gather("wbs", 0, 2, "h_rows0_1")
+        gather("was", 2, 3, "waw_g0")
+        gather("wbs", 0, 2)
+        gather("wbw", 0, 2)
         quantize(0, 2)
-        gather("wbw", 2, 4, "waw_g1")
-        gather("wbs", 2, 4, "waw_g0")
-        turn(2, "a")
-        turn(3, "d")
-        y001 = y_out(second_layer((0,), 0, 2, "c"), 0, 2 * P, "y001")
-        quantize(2, 4)
-        yt = sb("yt", TURNED * P, F32)
-        gated_rows(1, 0, 2, "d", yt)
-        y13 = y_out(second_layer((1,), 3, 4, "a"), 0, P, "y13")
-        y023 = y_out(second_layer((0,), 2, 4, "b"), 0, 2 * P, "y023")
-        gated_rows(1, 2, 3, "c", yt)
-        back_ps = bank("back_ps", "b")
-        for m in range(TURNED):
-            nc.tensor.transpose(back_ps[:, P * m : P * m + P], yt[:, P * m : P * m + P], ident[:])
-        gated = y_out(back_ps, 0, TURNED * P, "gated")
-        early_ps = bank("base0_early", "c")
-        frozen(0, 0, 2 * P, early_ps)
-        base0 = y_out(frozen(0, 2 * P, SPLIT, early_ps), 0, SPLIT, "base0")
-        base0_ps = frozen(0, SPLIT, T, bank("base0_late", "b"))
-        base1_ps = frozen(1, 0, T, bank("base1", "c"))
-        scatter(0, 0, 2, y001[:])
-        scatter(1, 3, 4, y13[:])
-        scatter(0, 2, 4, y023[:])
-        nc.vector.tensor_copy(out=placed[1][:].indirect(tok_list[:, 0 : TURNED * P // 16]), in_=gated[:])
-        res0a = sb("res0a", SPLIT, F32)
-        res0b = sb("res0b", T - SPLIT, F32)
-        res1 = sb("res1", T, F32)
-        nc.gpsimd.tensor_tensor(out=res0a[:], in0=base0[:], in1=placed[0][:, 0:SPLIT], op=ADD)
-        nc.scalar.dma_start(out=out[0:P, 0:SPLIT], in_=res0a[:])
-        nc.vector.tensor_tensor(out=res0b[:], in0=base0_ps[:, SPLIT:T], in1=placed[0][:, SPLIT:T], op=ADD)
-        nc.sync.dma_start(out=out[0:P, SPLIT:T], in_=res0b[:])
-        for lo in (0, T // 2):
-            hi = lo + T // 2
-            nc.vector.tensor_tensor(out=res1[:, lo:hi], in0=base1_ps[:, lo:hi], in1=placed[1][:, lo:hi], op=ADD)
-            nc.sync.dma_start(out=out[P : 2 * P, lo:hi], in_=res1[:, lo:hi])
+        second_layer(0, 2, "y0")
+        gather("xs", 2, 4, 0)
+        gather("was", 3, 4, 512)
+        gated(0, 2)
+        for m in range(2):
+            for c in range(2):
+                scatter(m, m + 1, c)
+        gather("waw", 2, 3, "hs0")
+        first_layer(2, "c")
+        gather("waw", 3, 4, "hq0")
+        first_layer(3, "d")
+        gather("wbs", 2, 4, "wbs_g0")
+        gather("wbw", 2, 4, "wbw_g0")
+        quantize(2, 3)
+        second_layer(2, 3, "y1")
+        quantize(3, 4)
+        second_layer(3, 4, "y0")
+        gated(2, 3)
+        gated(3, 4)
+        scatter(2, 3, 0, True)
+        scatter(2, 3, 1)
+        scatter(3, 4, 0, True)
+        scatter(3, 4, 1)
+        base = [frozen(c) for c in range(2)]
+        for c in range(2):
+            for lo in (0, T // 2):
+                finish(c, lo, lo + T // 2, base[c], nc.sync)

@@ -1,6 +1,7 @@
 from contextlib import ExitStack
 
 import concourse.mybir as mybir
+from concourse.masks import make_identity
 
 K, T, E, B, H, N = 512, 512, 4, 4, 512, 256
 P = 128
@@ -50,6 +51,7 @@ def tile_moe_dyl_gelu_kernel(
         wbw, wbs = sb("wbw", E * N, I32), sb("wbs", E * N, U8)
         ww, ws = sb("ww", 2 * N, U8), sb("ws", N, U8)
         gate_sb = sb("gate_sb", T, F32)
+        ident = sb("ident", P, F32)
         placed = [sb("placed%d" % c, T, F32) for c in range(2)]
 
         def load_words(tile, words, lo, hi, queue=nc.sync):
@@ -64,6 +66,8 @@ def tile_moe_dyl_gelu_kernel(
         for plane in (was, xs, wbs, ws):
             nc.vector.memset(plane[:].bitcast(I32), 0)
         nc.vector.memset(xw[:, T:TOKEN_WINDOW], 0)
+        nc.vector.memset(ident[:], 0.0)
+        make_identity(nc, ident[:], nomemset=True)
 
         load_words(xw, x_words, 0, T, nc.scalar)
         nc.sync.dma_start(tok_list[:], offs)
@@ -96,27 +100,34 @@ def tile_moe_dyl_gelu_kernel(
         def gather(kind, m0, m1, slot=None):
             window, lst, width, dtype = sources[kind]
             tile = sb("%s_g%d" % (kind, m0), width * (m1 - m0), dtype, slot)
-            target = tile[:]
-            if lst is wa_list:
-                target = target.rearrange("p (m t q) -> p m q t", t=4, q=P)
-            nc.vector.tensor_copy(out=target, in_=window.indirect(lst[:, width * m0 // 16 : width * m1 // 16]))
+            nc.vector.tensor_copy(out=tile[:], in_=window.indirect(lst[:, width * m0 // 16 : width * m1 // 16]))
             for m in range(m0, m1):
                 part[kind, m] = (tile, width * (m - m0))
 
         def first_layer(m, slot):
             h_ps = bank("h_ps%d" % m, slot)
-            for t in range(4):
-                nc.tensor.matmul_mx(
-                    out=h_ps[:, P * t : P * t + P],
-                    lhsT=view("waw", m, P * t, P * t + P).bitcast(FP8X4),
-                    lhsT_scale=view("was", m, P * t, P * t + P, WA_ROW),
-                    rhs=view("xw", m, 0, P).bitcast(FP8X4), rhs_scale=view("xs", m, 0, P),
-                    start=True, stop=True,
+            nc.tensor.matmul_mx(
+                out=h_ps[:],
+                lhsT=view("xw", m, 0, P).bitcast(FP8X4), lhsT_scale=view("xs", m, 0, P),
+                rhs=view("waw", m, 0, H).bitcast(FP8X4), rhs_scale=view("was", m, 0, H, WA_ROW),
+                start=True, stop=True,
+            )
+            for u in range(2):
+                h_rows = sb("h_rows%d_%d" % (m, u), H // 2, BF16)
+                nc.scalar.activation(
+                    out=h_rows[:].rearrange("s (p e) -> s p e", e=2),
+                    in_=h_ps[:].rearrange("s (p u e) -> s u p e", u=2, e=2)[:, u],
+                    func=GELU,
                 )
-            nc.scalar.activation(
-                out=view("h", m, 0, H).rearrange("p (s t) -> p s t", t=4),
-                in_=h_ps[:].rearrange("p (t s) -> p s t", t=4),
-                func=GELU,
+                part["h_rows", m, u] = h_rows
+
+        def turn(m, slot):
+            t_ps = bank("t_ps%d" % m, slot)
+            for u in range(2):
+                nc.tensor.transpose(t_ps[:, P * u : P * u + P], part["h_rows", m, u][:].bitcast(F32), ident[:])
+            nc.scalar.copy(
+                out=view("h", m, 0, H).bitcast(F32).rearrange("p (s u) -> p s u", u=2),
+                in_=t_ps[:, 0 : 2 * P].rearrange("p (u s) -> p s u", u=2),
             )
 
         def new(kind, m0, m1, width, dtype, slot=None):
@@ -181,37 +192,42 @@ def tile_moe_dyl_gelu_kernel(
             nc.vector.tensor_tensor(out=res[:], in0=base_ps[:, lo:hi], in1=placed[c][:, lo:hi], op=ADD)
             queue.dma_start(out=out[P * c : P * c + P, lo:hi], in_=res[:])
 
-        new("h", 0, 2, H, BF16, 0)
-        new("h", 2, 3, H, BF16)
-        new("h", 3, 4, H, BF16)
+        new("h", 0, 2, H, BF16)
+        new("h", 2, 4, H, BF16)
         gather("xw", 0, 4)
         gather("was", 0, 2)
-        gather("xs", 0, 2)
+        gather("xs", 0, 4)
         gather("waw", 0, 1)
         first_layer(0, "a")
         gather("waw", 1, 2)
         first_layer(1, "b")
-        gather("was", 2, 3, "waw_g0")
-        gather("wbs", 0, 2)
-        gather("wbw", 0, 2)
+        turn(0, "c")
+        turn(1, "d")
+        gather("waw", 2, 3)
+        gather("was", 2, 4, "waw_g0")
+        gather("waw", 3, 4, "waw_g1")
+        first_layer(2, "b")
+        first_layer(3, "c")
+        gather("wbs", 0, 2, "was_g0")
+        gather("wbw", 0, 1, "h_rows0_1")
         quantize(0, 2)
-        second_layer(0, 2, "y0")
-        gather("xs", 2, 4, 0)
-        gather("was", 3, 4, 512)
-        gated(0, 2)
-        for m in range(2):
-            for c in range(2):
-                scatter(m, m + 1, c)
-        gather("waw", 2, 3, "hs0")
-        first_layer(2, "c")
-        gather("waw", 3, 4, "hq0")
-        first_layer(3, "d")
-        gather("wbs", 2, 4, "wbs_g0")
-        gather("wbw", 2, 4, "wbw_g0")
-        quantize(2, 3)
-        second_layer(2, 3, "y1")
-        quantize(3, 4)
-        second_layer(3, 4, "y0")
+        gather("wbw", 1, 2, "waw_g1")
+        gather("wbs", 2, 4, "waw_g0")
+        turn(2, "a")
+        turn(3, "d")
+        second_layer(0, 1, "a")
+        second_layer(1, 2, "d")
+        gated(0, 1)
+        scatter(0, 1, 0)
+        scatter(0, 1, 1)
+        gather("wbw", 2, 3, "h_rows0_1")
+        gated(1, 2)
+        quantize(2, 4, "hq0")
+        second_layer(2, 3, "y0")
+        gather("wbw", 3, 4, "hs0")
+        second_layer(3, 4, "y1")
+        scatter(1, 2, 0, True)
+        scatter(1, 2, 1)
         gated(2, 3)
         gated(3, 4)
         scatter(2, 3, 0, True)

@@ -52,7 +52,6 @@ def tile_moe_dyl_gelu_kernel(
         ww, ws = sb("ww", 2 * N, U8), sb("ws", N, U8)
         gate_sb = sb("gate_sb", T, F32)
         ident = sb("ident", P, F32)
-        placed = [sb("placed%d" % c, T, F32) for c in range(2)]
 
         def load_words(tile, words, lo, hi, queue=nc.sync):
             queue.dma_start(out=tile[:, lo:hi], in_=words[0, :, lo:hi, :].rearrange("p c d -> p (c d)").bitcast(I32))
@@ -113,7 +112,7 @@ def tile_moe_dyl_gelu_kernel(
                 start=True, stop=True,
             )
             for u in range(2):
-                h_rows = sb("h_rows%d_%d" % (m, u), H // 2, BF16)
+                h_rows = sb("h_rows%d_%d" % (m, u), H // 2, BF16, 4 * T - 256 if (m, u) == (3, 1) else None)
                 nc.scalar.activation(
                     out=h_rows[:].rearrange("s (p e) -> s p e", e=2),
                     in_=h_ps[:].rearrange("s (p u e) -> s u p e", u=2, e=2)[:, u],
@@ -216,15 +215,16 @@ def tile_moe_dyl_gelu_kernel(
         turn(2, "a")
         turn(3, "d")
         second_layer(0, 1, "a")
-        second_layer(1, 2, "d")
+        second_layer(1, 2, "c")
+        placed = [sb("placed%d" % c, T, F32, 4 * T * c) for c in range(2)]
         gated(0, 1)
         scatter(0, 1, 0)
         scatter(0, 1, 1)
         gather("wbw", 2, 3, "h_rows0_1")
         gated(1, 2)
+        gather("wbw", 3, 4, "hs0")
         quantize(2, 4, "hq0")
         second_layer(2, 3, "y0")
-        gather("wbw", 3, 4, "hs0")
         second_layer(3, 4, "y1")
         scatter(1, 2, 0, True)
         scatter(1, 2, 1)

@@ -24,6 +24,7 @@ WA_ROW = 4
 WB_ROW = 8
 TOKEN_WINDOW = 704
 WA_FIRST = 1280
+ROWS_AT = {(3, 1): 2048 - 256, (0, 1): 8192}
 
 
 def tile_moe_dyl_gelu_kernel(
@@ -112,7 +113,7 @@ def tile_moe_dyl_gelu_kernel(
                 start=True, stop=True,
             )
             for u in range(2):
-                h_rows = sb("h_rows%d_%d" % (m, u), H // 2, BF16, 4 * T - 256 if (m, u) == (3, 1) else None)
+                h_rows = sb("h_rows%d_%d" % (m, u), H // 2, BF16, ROWS_AT.get((m, u)))
                 nc.scalar.activation(
                     out=h_rows[:].rearrange("s (p e) -> s p e", e=2),
                     in_=h_ps[:].rearrange("s (p u e) -> s u p e", u=2, e=2)[:, u],
@@ -155,22 +156,18 @@ def tile_moe_dyl_gelu_kernel(
                     )
             part["y", m0] = y_ps
 
-        def gated(m0, m1):
-            width = P * (m1 - m0)
-            gy = sb("gy%d" % m0, 2 * width, F32)
+        def gated(m):
+            pair, first = part["gy", m]
             nc.vector.tensor_tensor(
-                out=gy[:].rearrange("p (c s) -> p c s", c=2),
-                in0=part["y", m0][:, 0 : 2 * width].rearrange("p (c s) -> p c s", c=2),
-                in1=gate_sb[:, P * m0 : P * m1].unsqueeze(1).to_broadcast([P, 2, width]),
+                out=pair[:].rearrange("p (c s) -> p c s", c=2)[:, :, first : first + P],
+                in0=part["y", m][:, 0:N].rearrange("p (c s) -> p c s", c=2),
+                in1=gate_sb[:, P * m : P * m + P].unsqueeze(1).to_broadcast([P, 2, P]),
                 op=MULT,
             )
-            for m in range(m0, m1):
-                for c in range(2):
-                    part[("gy", c), m] = (gy, width * c + P * (m - m0))
 
         def scatter(m0, m1, c, on_vector=False):
             target = placed[c][:].indirect(tok_list[:, P * m0 // 16 : P * m1 // 16])
-            values = view(("gy", c), m0, 0, P * (m1 - m0))
+            values = view("gy", m0, 2 * P * c, 2 * P * c + P * (m1 - m0))
             if on_vector:
                 nc.vector.tensor_copy(out=target, in_=values)
             else:
@@ -192,7 +189,12 @@ def tile_moe_dyl_gelu_kernel(
             queue.dma_start(out=out[P * c : P * c + P, lo:hi], in_=res[:])
 
         new("h", 0, 2, H, BF16)
-        new("h", 2, 4, H, BF16)
+        new("h", 2, 3, H, BF16)
+        new("h", 3, 4, H, BF16)
+        for m0 in (0, 2):
+            pair = sb("gy%d" % m0, 2 * N, F32)
+            for m in (m0, m0 + 1):
+                part["gy", m] = (pair, P * (m - m0))
         gather("xw", 0, 4)
         gather("was", 0, 2)
         gather("xs", 0, 4)
@@ -208,32 +210,30 @@ def tile_moe_dyl_gelu_kernel(
         first_layer(2, "b")
         first_layer(3, "c")
         gather("wbs", 0, 2, "was_g0")
-        gather("wbw", 0, 1, "h_rows0_1")
+        gather("wbw", 0, 1, 8192)
         quantize(0, 2)
         gather("wbw", 1, 2, "waw_g1")
         gather("wbs", 2, 4, "waw_g0")
         turn(2, "a")
         turn(3, "d")
-        second_layer(0, 1, "a")
+        second_layer(0, 1, "b")
         second_layer(1, 2, "c")
         placed = [sb("placed%d" % c, T, F32, 4 * T * c) for c in range(2)]
-        gated(0, 1)
+        gated(0)
         scatter(0, 1, 0)
-        scatter(0, 1, 1)
-        gather("wbw", 2, 3, "h_rows0_1")
-        gated(1, 2)
-        gather("wbw", 3, 4, "hs0")
-        quantize(2, 4, "hq0")
+        gather("wbw", 2, 3, 8192 - 512)
+        quantize(2, 3, 8192 + 512)
         second_layer(2, 3, "y0")
+        gated(1)
+        scatter(0, 2, 1)
+        gather("wbw", 3, 4, "hs0")
+        quantize(3, 4, "hq0")
         second_layer(3, 4, "y1")
+        gated(2)
         scatter(1, 2, 0, True)
-        scatter(1, 2, 1)
-        gated(2, 3)
-        gated(3, 4)
-        scatter(2, 3, 0, True)
-        scatter(2, 3, 1)
-        scatter(3, 4, 0, True)
-        scatter(3, 4, 1)
+        gated(3)
+        scatter(2, 4, 0, True)
+        scatter(2, 4, 1)
         base = [frozen(c) for c in range(2)]
         for c in range(2):
             for lo in (0, T // 2):

@@ -24,6 +24,7 @@ WA_ROW = 4
 WB_ROW = 8
 TOKEN_WINDOW = 704
 WA_FIRST = 1280
+SPLIT = 256
 ROWS_AT = {(3, 1): 2048 - 256, (0, 1): 8192}
 
 
@@ -63,7 +64,8 @@ def tile_moe_dyl_gelu_kernel(
                     out=tile[row + r : P : 32, 0 : scales.shape[2]].bitcast(I32), in_=scales[0, r:16:4, :].bitcast(I32)
                 )
 
-        for plane in (was, xs, wbs, ws):
+        nc.gpsimd.memset(ws[:].bitcast(I32), 0)
+        for plane in (was, xs, wbs):
             nc.vector.memset(plane[:].bitcast(I32), 0)
         nc.vector.memset(xw[:, T:TOKEN_WINDOW], 0)
         nc.vector.memset(ident[:], 0.0)
@@ -80,8 +82,8 @@ def tile_moe_dyl_gelu_kernel(
         load_words(wbw, wb_words, 0, E * N)
         load_scales(wbs, wb_scales, WB_ROW)
         nc.sync.dma_start(out=gate_sb[:], in_=gate)
-        nc.sync.dma_start(out=ww[:].bitcast(I32), in_=w_words[0].bitcast(I32))
-        load_scales(ws, w_scales, 0)
+        nc.gpsimd.dma_start(out=ww[:].bitcast(I32), in_=w_words[0].bitcast(I32))
+        load_scales(ws, w_scales, 0, nc.gpsimd)
 
         sources = {
             "xw": (xw[:].bitcast(U32), tok_list, P, U32),
@@ -183,9 +185,9 @@ def tile_moe_dyl_gelu_kernel(
             )
             return base_ps
 
-        def finish(c, lo, hi, base_ps, queue):
+        def finish(c, lo, hi, base_ps, queue, engine=nc.vector):
             res = sb("res%d_%d" % (c, lo), hi - lo, F32)
-            nc.vector.tensor_tensor(out=res[:], in0=base_ps[:, lo:hi], in1=placed[c][:, lo:hi], op=ADD)
+            engine.tensor_tensor(out=res[:], in0=base_ps[:, lo:hi], in1=placed[c][:, lo:hi], op=ADD)
             queue.dma_start(out=out[P * c : P * c + P, lo:hi], in_=res[:])
 
         new("h", 0, 2, H, BF16)
@@ -235,6 +237,9 @@ def tile_moe_dyl_gelu_kernel(
         scatter(2, 4, 0, True)
         scatter(2, 4, 1)
         base = [frozen(c) for c in range(2)]
-        for c in range(2):
-            for lo in (0, T // 2):
-                finish(c, lo, lo + T // 2, base[c], nc.sync)
+        base_sb = sb("base_sb", SPLIT, F32)
+        nc.scalar.copy(out=base_sb[:], in_=base[0][:, 0:SPLIT])
+        finish(0, SPLIT, T, base[0], nc.sync)
+        finish(0, 0, SPLIT, base_sb, nc.scalar, nc.gpsimd)
+        finish(1, 0, T // 2, base[1], nc.sync)
+        finish(1, T // 2, T, base[1], nc.sync)

@@ -175,12 +175,12 @@ def tile_moe_dyl_gelu_kernel(
             else:
                 nc.scalar.activation(out=target, in_=values, func=COPY)
 
-        def frozen(c):
-            base_ps = bank("base%d" % c, "base%d" % c)
+        def frozen(c, lo, hi, slot):
+            base_ps = bank("base%d_%d" % (c, lo), slot)
             nc.tensor.matmul_mx(
-                out=base_ps[:],
+                out=base_ps[:, lo:hi],
                 lhsT=ww[:, 2 * P * c : 2 * P * c + 2 * P].bitcast(FP4X4), lhsT_scale=ws[:, P * c : P * c + P],
-                rhs=xw[:, 0:T].bitcast(FP8X4), rhs_scale=xs[:, 0:T],
+                rhs=xw[:, lo:hi].bitcast(FP8X4), rhs_scale=xs[:, lo:hi],
                 start=True, stop=True,
             )
             return base_ps
@@ -217,7 +217,7 @@ def tile_moe_dyl_gelu_kernel(
         gather("wbw", 1, 2, "waw_g1")
         gather("wbs", 2, 4, "waw_g0")
         turn(2, "a")
-        turn(3, "d")
+        turn(3, "f")
         second_layer(0, 1, "b")
         second_layer(1, 2, "c")
         placed = [sb("placed%d" % c, T, F32, 4 * T * c) for c in range(2)]
@@ -236,10 +236,11 @@ def tile_moe_dyl_gelu_kernel(
         gated(3)
         scatter(2, 4, 0, True)
         scatter(2, 4, 1)
-        base = [frozen(c) for c in range(2)]
+        base0 = frozen(0, 0, T, "e")
         base_sb = sb("base_sb", SPLIT, F32)
-        nc.scalar.copy(out=base_sb[:], in_=base[0][:, 0:SPLIT])
-        finish(0, SPLIT, T, base[0], nc.sync)
+        nc.scalar.copy(out=base_sb[:], in_=base0[:, 0:SPLIT])
+        base1 = frozen(1, 0, T, "d")
+        finish(0, SPLIT, T, base0, nc.sync)
         finish(0, 0, SPLIT, base_sb, nc.scalar, nc.gpsimd)
-        finish(1, 0, T // 2, base[1], nc.sync)
-        finish(1, T // 2, T, base[1], nc.sync)
+        finish(1, 0, T // 2, base1, nc.sync)
+        finish(1, T // 2, T, base1, nc.sync)

@@ -191,8 +191,7 @@ def tile_moe_dyl_gelu_kernel(
             queue.dma_start(out=out[P * c : P * c + P, lo:hi], in_=res[:])
 
         new("h", 0, 2, H, BF16)
-        new("h", 2, 3, H, BF16)
-        new("h", 3, 4, H, BF16)
+        new("h", 2, 4, H, BF16)
         for m0 in (0, 2):
             pair = sb("gy%d" % m0, 2 * N, F32)
             for m in (m0, m0 + 1):
@@ -214,8 +213,7 @@ def tile_moe_dyl_gelu_kernel(
         gather("wbs", 0, 2, "was_g0")
         gather("wbw", 0, 1, 8192)
         quantize(0, 2)
-        gather("wbw", 1, 2, "waw_g1")
-        gather("wbs", 2, 4, "waw_g0")
+        gather("wbw", 1, 4, "waw_g1")
         turn(2, "a")
         turn(3, "f")
         second_layer(0, 1, "b")
@@ -223,16 +221,14 @@ def tile_moe_dyl_gelu_kernel(
         placed = [sb("placed%d" % c, T, F32, 4 * T * c) for c in range(2)]
         gated(0)
         scatter(0, 1, 0)
-        gather("wbw", 2, 3, 8192 - 512)
-        quantize(2, 3, 8192 + 512)
-        second_layer(2, 3, "y0")
+        gather("wbs", 2, 4, 8192)
         gated(1)
         scatter(0, 2, 1)
-        gather("wbw", 3, 4, "hs0")
-        quantize(3, 4, "hq0")
+        quantize(2, 4, "hq0")
+        second_layer(2, 3, "y0")
         second_layer(3, 4, "y1")
-        gated(2)
         scatter(1, 2, 0, True)
+        gated(2)
         gated(3)
         scatter(2, 4, 0, True)
         scatter(2, 4, 1)

@@ -167,6 +167,13 @@ def tile_moe_dyl_gelu_kernel(
                 op=MULT,
             )
 
+        def gated_half(m, c):
+            pair, first = part["gy", m]
+            at = N * c + first
+            nc.vector.tensor_tensor(
+                out=pair[:, at : at + P], in0=part["y", m][:, P * c : P * c + P], in1=gate_sb[:, P * m : P * m + P], op=MULT
+            )
+
         def scatter(m0, m1, c, on_vector=False):
             target = placed[c][:].indirect(tok_list[:, P * m0 // 16 : P * m1 // 16])
             values = view("gy", m0, 2 * P * c, 2 * P * c + P * (m1 - m0))
@@ -229,7 +236,8 @@ def tile_moe_dyl_gelu_kernel(
         second_layer(3, 4, "y1")
         scatter(1, 2, 0, True)
         gated(2)
-        gated(3)
+        gated_half(3, 0)
+        gated_half(3, 1)
         scatter(2, 4, 0, True)
         scatter(2, 4, 1)
         base0 = frozen(0, 0, T, "e")

@@ -25,7 +25,7 @@ WB_ROW = 8
 TOKEN_WINDOW = 704
 WA_FIRST = 1280
 SPLIT = 256
-ROWS_AT = {(3, 1): 2048 - 256, (0, 1): 8192}
+KIB = 1024
 
 
 def tile_moe_dyl_gelu_kernel(
@@ -37,10 +37,10 @@ def tile_moe_dyl_gelu_kernel(
         shared = ctx.enter_context(tc.tile_pool(name="shared", bufs=1))
         psum = ctx.enter_context(tc.psum_pool(name="psum", bufs=1))
 
-        def sb(name, cols, dtype, slot=None):
-            if isinstance(slot, int):
-                return shared.tile([P, cols], dtype, name=name, align_bytes=64, offset=slot)
-            return keep.tile([P, cols], dtype, name=name, tag=slot or name, align_bytes=64)
+        def sb(name, cols, dtype, at=None):
+            if at is None:
+                return keep.tile([P, cols], dtype, name=name, align_bytes=64)
+            return shared.tile([P, cols], dtype, name=name, align_bytes=64, offset=at)
 
         def bank(name, slot):
             return psum.tile([P, 512], F32, name=name, tag=slot)
@@ -64,6 +64,112 @@ def tile_moe_dyl_gelu_kernel(
                     out=tile[row + r : P : 32, 0 : scales.shape[2]].bitcast(I32), in_=scales[0, r:16:4, :].bitcast(I32)
                 )
 
+        sources = {
+            "xw": (xw[:].bitcast(U32), tok_list, P, U32),
+            "xs": (xs[:], tok_list, P, U8),
+            "waw": (waw[:].bitcast(U32), wa_list, H, U32),
+            "was": (was[:], wa_list, H, U8),
+            "wbw": (wbw[:].bitcast(U32), wb_list, N, U32),
+            "wbs": (wbs[:], wb_list, N, U8),
+        }
+        part = {}
+
+        def new(kind, m0, m1, width, dtype, at=None):
+            tile = sb("%s_%d" % (kind, m0), width * (m1 - m0), dtype, at)
+            for m in range(m0, m1):
+                part[kind, m] = (tile, width * (m - m0))
+            return tile
+
+        def view(kind, m, lo, hi, row=0):
+            tile, first = part[kind, m]
+            return tile[row:P, first + lo : first + hi]
+
+        def gather(kind, m0, m1, at=None):
+            window, lst, width, dtype = sources[kind]
+            tile = new(kind + "g", m0, m1, width, dtype, at)
+            nc.vector.tensor_copy(out=tile[:], in_=window.indirect(lst[:, width * m0 // 16 : width * m1 // 16]))
+
+        def first_layer(m, slot, rows_at=None):
+            h_ps = bank("h_ps%d" % m, slot)
+            nc.tensor.matmul_mx(
+                out=h_ps[:],
+                lhsT=view("xwg", m, 0, P).bitcast(FP8X4), lhsT_scale=view("xsg", m, 0, P),
+                rhs=view("wawg", m, 0, H).bitcast(FP8X4), rhs_scale=view("wasg", m, 0, H, WA_ROW),
+                start=True, stop=True,
+            )
+            for u in range(2):
+                rows = new("rows%d" % u, m, m + 1, H // 2, BF16, rows_at if u == 1 else None)
+                nc.scalar.activation(
+                    out=rows[:].rearrange("s (p e) -> s p e", e=2),
+                    in_=h_ps[:].rearrange("s (p u e) -> s u p e", u=2, e=2)[:, u],
+                    func=GELU,
+                )
+
+        def turn(m, slot):
+            t_ps = bank("t_ps%d" % m, slot)
+            for u in range(2):
+                nc.tensor.transpose(t_ps[:, P * u : P * u + P], view("rows%d" % u, m, 0, H // 2).bitcast(F32), ident[:])
+            nc.scalar.copy(
+                out=view("h", m, 0, H).bitcast(F32).rearrange("p (s u) -> p s u", u=2),
+                in_=t_ps[:, 0 : 2 * P].rearrange("p (u s) -> p s u", u=2),
+            )
+
+        def quantize(m0, m1, at=None, scales_at=None):
+            hq = new("hq", m0, m1, P, U32, at)
+            hs = new("hs", m0, m1, P, U8, scales_at)
+            nc.vector.quantize_mx(out=hq[:].bitcast(FP8X4), scales=hs[:], in_=view("h", m0, 0, H * (m1 - m0)))
+
+        def second_layer(m, slot):
+            y_ps = bank("y_ps%d" % m, slot)
+            for c in range(2):
+                nc.tensor.matmul_mx(
+                    out=y_ps[:, P * c : P * c + P],
+                    lhsT=view("wbwg", m, P * c, P * c + P).bitcast(FP8X4),
+                    lhsT_scale=view("wbsg", m, P * c, P * c + P, WB_ROW),
+                    rhs=view("hq", m, 0, P).bitcast(FP8X4), rhs_scale=view("hs", m, 0, P),
+                    start=True, stop=True,
+                )
+            part["y", m] = y_ps
+
+        def gated(m):
+            pair, first = part["gy", m]
+            nc.vector.tensor_tensor(
+                out=pair[:].rearrange("p (c s) -> p c s", c=2)[:, :, first : first + P],
+                in0=part["y", m][:, 0:N].rearrange("p (c s) -> p c s", c=2),
+                in1=gate_sb[:, P * m : P * m + P].unsqueeze(1).to_broadcast([P, 2, P]),
+                op=MULT,
+            )
+
+        def gated_half(m, c):
+            pair, first = part["gy", m]
+            at = N * c + first
+            nc.vector.tensor_tensor(
+                out=pair[:, at : at + P], in0=part["y", m][:, P * c : P * c + P], in1=gate_sb[:, P * m : P * m + P], op=MULT
+            )
+
+        def scatter(m0, m1, c, on_vector=False):
+            target = placed[c][:].indirect(tok_list[:, P * m0 // 16 : P * m1 // 16])
+            values = view("gy", m0, N * c, N * c + P * (m1 - m0))
+            if on_vector:
+                nc.vector.tensor_copy(out=target, in_=values)
+            else:
+                nc.scalar.activation(out=target, in_=values, func=COPY)
+
+        def frozen(c, lo, hi, slot):
+            base_ps = bank("base%d_%d" % (c, lo), slot)
+            nc.tensor.matmul_mx(
+                out=base_ps[:, lo:hi],
+                lhsT=ww[:, 2 * P * c : 2 * P * c + 2 * P].bitcast(FP4X4), lhsT_scale=ws[:, P * c : P * c + P],
+                rhs=xw[:, lo:hi].bitcast(FP8X4), rhs_scale=xs[:, lo:hi],
+                start=True, stop=True,
+            )
+            return base_ps
+
+        def finish(c, lo, hi, base, queue, engine=nc.vector):
+            res = sb("res%d_%d" % (c, lo), hi - lo, F32)
+            engine.tensor_tensor(out=res[:], in0=base[:, lo:hi], in1=placed[c][:, lo:hi], op=ADD)
+            queue.dma_start(out=out[P * c : P * c + P, lo:hi], in_=res[:])
+
         nc.gpsimd.memset(ws[:].bitcast(I32), 0)
         for plane in (was, xs, wbs):
             nc.vector.memset(plane[:].bitcast(I32), 0)
@@ -85,118 +191,6 @@ def tile_moe_dyl_gelu_kernel(
         nc.gpsimd.dma_start(out=ww[:].bitcast(I32), in_=w_words[0].bitcast(I32))
         load_scales(ws, w_scales, 0, nc.gpsimd)
 
-        sources = {
-            "xw": (xw[:].bitcast(U32), tok_list, P, U32),
-            "xs": (xs[:], tok_list, P, U8),
-            "waw": (waw[:].bitcast(U32), wa_list, H, U32),
-            "was": (was[:], wa_list, H, U8),
-            "wbw": (wbw[:].bitcast(U32), wb_list, N, U32),
-            "wbs": (wbs[:], wb_list, N, U8),
-        }
-        part = {}
-
-        def view(kind, m, lo, hi, row=0):
-            tile, first = part[kind, m]
-            return tile[row:P, first + lo : first + hi]
-
-        def gather(kind, m0, m1, slot=None):
-            window, lst, width, dtype = sources[kind]
-            tile = sb("%s_g%d" % (kind, m0), width * (m1 - m0), dtype, slot)
-            nc.vector.tensor_copy(out=tile[:], in_=window.indirect(lst[:, width * m0 // 16 : width * m1 // 16]))
-            for m in range(m0, m1):
-                part[kind, m] = (tile, width * (m - m0))
-
-        def first_layer(m, slot):
-            h_ps = bank("h_ps%d" % m, slot)
-            nc.tensor.matmul_mx(
-                out=h_ps[:],
-                lhsT=view("xw", m, 0, P).bitcast(FP8X4), lhsT_scale=view("xs", m, 0, P),
-                rhs=view("waw", m, 0, H).bitcast(FP8X4), rhs_scale=view("was", m, 0, H, WA_ROW),
-                start=True, stop=True,
-            )
-            for u in range(2):
-                h_rows = sb("h_rows%d_%d" % (m, u), H // 2, BF16, ROWS_AT.get((m, u)))
-                nc.scalar.activation(
-                    out=h_rows[:].rearrange("s (p e) -> s p e", e=2),
-                    in_=h_ps[:].rearrange("s (p u e) -> s u p e", u=2, e=2)[:, u],
-                    func=GELU,
-                )
-                part["h_rows", m, u] = h_rows
-
-        def turn(m, slot):
-            t_ps = bank("t_ps%d" % m, slot)
-            for u in range(2):
-                nc.tensor.transpose(t_ps[:, P * u : P * u + P], part["h_rows", m, u][:].bitcast(F32), ident[:])
-            nc.scalar.copy(
-                out=view("h", m, 0, H).bitcast(F32).rearrange("p (s u) -> p s u", u=2),
-                in_=t_ps[:, 0 : 2 * P].rearrange("p (u s) -> p s u", u=2),
-            )
-
-        def new(kind, m0, m1, width, dtype, slot=None):
-            tile = sb("%s%d" % (kind, m0), width * (m1 - m0), dtype, slot)
-            for m in range(m0, m1):
-                part[kind, m] = (tile, width * (m - m0))
-            return tile
-
-        def quantize(m0, m1, hq_slot=None):
-            hq = new("hq", m0, m1, P, U32, hq_slot)
-            hs = new("hs", m0, m1, P, U8)
-            nc.vector.quantize_mx(out=hq[:].bitcast(FP8X4), scales=hs[:], in_=view("h", m0, 0, H * (m1 - m0)))
-
-        def second_layer(m0, m1, slot):
-            y_ps = bank("y_ps%d" % m0, slot)
-            width = P * (m1 - m0)
-            for m in range(m0, m1):
-                for c in range(2):
-                    at = width * c + P * (m - m0)
-                    nc.tensor.matmul_mx(
-                        out=y_ps[:, at : at + P],
-                        lhsT=view("wbw", m, P * c, P * c + P).bitcast(FP8X4),
-                        lhsT_scale=view("wbs", m, P * c, P * c + P, WB_ROW),
-                        rhs=view("hq", m, 0, P).bitcast(FP8X4), rhs_scale=view("hs", m, 0, P),
-                        start=True, stop=True,
-                    )
-            part["y", m0] = y_ps
-
-        def gated(m):
-            pair, first = part["gy", m]
-            nc.vector.tensor_tensor(
-                out=pair[:].rearrange("p (c s) -> p c s", c=2)[:, :, first : first + P],
-                in0=part["y", m][:, 0:N].rearrange("p (c s) -> p c s", c=2),
-                in1=gate_sb[:, P * m : P * m + P].unsqueeze(1).to_broadcast([P, 2, P]),
-                op=MULT,
-            )
-
-        def gated_half(m, c):
-            pair, first = part["gy", m]
-            at = N * c + first
-            nc.vector.tensor_tensor(
-                out=pair[:, at : at + P], in0=part["y", m][:, P * c : P * c + P], in1=gate_sb[:, P * m : P * m + P], op=MULT
-            )
-
-        def scatter(m0, m1, c, on_vector=False):
-            target = placed[c][:].indirect(tok_list[:, P * m0 // 16 : P * m1 // 16])
-            values = view("gy", m0, 2 * P * c, 2 * P * c + P * (m1 - m0))
-            if on_vector:
-                nc.vector.tensor_copy(out=target, in_=values)
-            else:
-                nc.scalar.activation(out=target, in_=values, func=COPY)
-
-        def frozen(c, lo, hi, slot):
-            base_ps = bank("base%d_%d" % (c, lo), slot)
-            nc.tensor.matmul_mx(
-                out=base_ps[:, lo:hi],
-                lhsT=ww[:, 2 * P * c : 2 * P * c + 2 * P].bitcast(FP4X4), lhsT_scale=ws[:, P * c : P * c + P],
-                rhs=xw[:, lo:hi].bitcast(FP8X4), rhs_scale=xs[:, lo:hi],
-                start=True, stop=True,
-            )
-            return base_ps
-
-        def finish(c, lo, hi, base_ps, queue, engine=nc.vector):
-            res = sb("res%d_%d" % (c, lo), hi - lo, F32)
-            engine.tensor_tensor(out=res[:], in0=base_ps[:, lo:hi], in1=placed[c][:, lo:hi], op=ADD)
-            queue.dma_start(out=out[P * c : P * c + P, lo:hi], in_=res[:])
-
         new("h", 0, 2, H, BF16)
         new("h", 2, 4, H, BF16)
         for m0 in (0, 2):
@@ -204,36 +198,36 @@ def tile_moe_dyl_gelu_kernel(
             for m in (m0, m0 + 1):
                 part["gy", m] = (pair, P * (m - m0))
         gather("xw", 0, 4)
-        gather("was", 0, 2)
+        gather("was", 0, 2, 8 * KIB)
         gather("xs", 0, 4)
-        gather("waw", 0, 1)
-        first_layer(0, "a")
-        gather("waw", 1, 2)
+        gather("waw", 0, 1, 0)
+        first_layer(0, "a", 9 * KIB)
+        gather("waw", 1, 2, 2 * KIB)
         first_layer(1, "b")
         turn(0, "c")
         turn(1, "d")
         gather("waw", 2, 3)
-        gather("was", 2, 4, "waw_g0")
-        gather("waw", 3, 4, "waw_g1")
+        gather("was", 2, 4, 0)
+        gather("waw", 3, 4, 2 * KIB)
         first_layer(2, "b")
-        first_layer(3, "c")
-        gather("wbs", 0, 2, "was_g0")
-        gather("wbw", 0, 1, 8192)
-        quantize(0, 2)
-        gather("wbw", 1, 4, "waw_g1")
+        first_layer(3, "c", 12 * KIB - 256)
+        gather("wbs", 0, 2, 8 * KIB)
+        gather("wbw", 0, 1, 9 * KIB)
+        quantize(0, 2, 14 * KIB)
+        gather("wbw", 1, 4, 2 * KIB)
         turn(2, "a")
         turn(3, "f")
-        second_layer(0, 1, "b")
-        second_layer(1, 2, "c")
-        placed = [sb("placed%d" % c, T, F32, 4 * T * c) for c in range(2)]
+        second_layer(0, "b")
+        placed = [sb("placed%d" % c, T, F32, (10 + 2 * c) * KIB) for c in range(2)]
         gated(0)
         scatter(0, 1, 0)
-        gather("wbs", 2, 4, 8192)
+        gather("wbs", 2, 4, 9 * KIB)
+        second_layer(1, "c")
         gated(1)
         scatter(0, 2, 1)
-        quantize(2, 4, "hq0")
-        second_layer(2, 3, "y0")
-        second_layer(3, 4, "y1")
+        quantize(2, 4, 14 * KIB)
+        second_layer(2, "g")
+        second_layer(3, "h")
         scatter(1, 2, 0, True)
         gated(2)
         gated_half(3, 0)
@@ -241,7 +235,7 @@ def tile_moe_dyl_gelu_kernel(
         scatter(2, 4, 0, True)
         scatter(2, 4, 1)
         base0 = frozen(0, 0, T, "e")
-        base_sb = sb("base_sb", SPLIT, F32)
+        base_sb = sb("base_sb", SPLIT, F32, 14 * KIB)
         nc.scalar.copy(out=base_sb[:], in_=base0[:, 0:SPLIT])
         base1 = frozen(1, 0, T, "d")
         finish(0, SPLIT, T, base0, nc.sync)

@@ -89,7 +89,7 @@ def tile_moe_dyl_gelu_kernel(
             tile = new(kind + "g", m0, m1, width, dtype, at)
             nc.vector.tensor_copy(out=tile[:], in_=window.indirect(lst[:, width * m0 // 16 : width * m1 // 16]))
 
-        def first_layer(m, slot, rows_at=None):
+        def first_layer(m, slot, rows_at=None, first_rows_at=None):
             h_ps = bank("h_ps%d" % m, slot)
             nc.tensor.matmul_mx(
                 out=h_ps[:],
@@ -98,12 +98,29 @@ def tile_moe_dyl_gelu_kernel(
                 start=True, stop=True,
             )
             for u in range(2):
-                rows = new("rows%d" % u, m, m + 1, H // 2, BF16, rows_at if u == 1 else None)
+                rows = new("rows%d" % u, m, m + 1, H // 2, BF16, rows_at if u == 1 else first_rows_at)
                 nc.scalar.activation(
                     out=rows[:].rearrange("s (p e) -> s p e", e=2),
                     in_=h_ps[:].rearrange("s (p u e) -> s u p e", u=2, e=2)[:, u],
                     func=GELU,
                 )
+
+        def first_layer_whole(m, slot, rows_at):
+            h_ps = bank("h_ps%d" % m, slot)
+            nc.tensor.matmul_mx(
+                out=h_ps[:],
+                lhsT=view("xwg", m, 0, P).bitcast(FP8X4), lhsT_scale=view("xsg", m, 0, P),
+                rhs=view("wawg", m, 0, H).bitcast(FP8X4), rhs_scale=view("wasg", m, 0, H, WA_ROW),
+                start=True, stop=True,
+            )
+            rows = new("rows", m, m + 1, H, BF16, rows_at)
+            nc.scalar.activation(
+                out=rows[:].rearrange("s (u p e) -> s u p e", u=2, e=2),
+                in_=h_ps[:].rearrange("s (p u e) -> s u p e", u=2, e=2),
+                func=GELU,
+            )
+            for u in range(2):
+                part["rows%d" % u, m] = (rows, N * u)
 
         def turn(m, slot):
             t_ps = bank("t_ps%d" % m, slot)
@@ -130,6 +147,24 @@ def tile_moe_dyl_gelu_kernel(
                     start=True, stop=True,
                 )
             part["y", m] = y_ps
+
+        def second_layer_half(m0, c, slot):
+            y_ps = bank("y_ps%d_%d" % (m0, c), slot)
+            for m in (m0, m0 + 1):
+                nc.tensor.matmul_mx(
+                    out=y_ps[:, P * (m - m0) : P * (m - m0) + P],
+                    lhsT=view("wbwg", m, P * c, P * c + P).bitcast(FP8X4),
+                    lhsT_scale=view("wbsg", m, P * c, P * c + P, WB_ROW),
+                    rhs=view("hq", m, 0, P).bitcast(FP8X4), rhs_scale=view("hs", m, 0, P),
+                    start=True, stop=True,
+                )
+            part["y", m0, c] = y_ps
+
+        def gated_pair(m0, c):
+            nc.vector.tensor_tensor(
+                out=view("gy", m0, N * c, N * c + N), in0=part["y", m0, c][:, 0:N],
+                in1=gate_sb[:, P * m0 : P * m0 + N], op=MULT,
+            )
 
         def gated(m):
             pair, first = part["gy", m]
@@ -170,8 +205,8 @@ def tile_moe_dyl_gelu_kernel(
             engine.tensor_tensor(out=res[:], in0=base[:, lo:hi], in1=placed[c][:, lo:hi], op=ADD)
             queue.dma_start(out=out[P * c : P * c + P, lo:hi], in_=res[:])
 
-        nc.gpsimd.memset(ws[:].bitcast(I32), 0)
-        for plane in (was, xs, wbs):
+        nc.gpsimd.memset(wbs[:].bitcast(I32), 0)
+        for plane in (was, xs, ws):
             nc.vector.memset(plane[:].bitcast(I32), 0)
         nc.vector.memset(xw[:, T:TOKEN_WINDOW], 0)
         nc.vector.memset(ident[:], 0.0)
@@ -184,12 +219,12 @@ def tile_moe_dyl_gelu_kernel(
         load_words(waw, wa_words, 0, WA_FIRST)
         load_scales(xs, x_scales, 0)
         load_words(waw, wa_words, WA_FIRST, E * H)
+        nc.gpsimd.dma_start(out=ww[:].bitcast(I32), in_=w_words[0].bitcast(I32))
+        load_scales(ws, w_scales, 0)
         nc.sync.dma_start(wb_list[:], offs3)
         load_words(wbw, wb_words, 0, E * N)
-        load_scales(wbs, wb_scales, WB_ROW)
+        load_scales(wbs, wb_scales, WB_ROW, nc.gpsimd)
         nc.sync.dma_start(out=gate_sb[:], in_=gate)
-        nc.gpsimd.dma_start(out=ww[:].bitcast(I32), in_=w_words[0].bitcast(I32))
-        load_scales(ws, w_scales, 0, nc.gpsimd)
 
         new("h", 0, 2, H, BF16)
         new("h", 2, 4, H, BF16)
@@ -226,12 +261,11 @@ def tile_moe_dyl_gelu_kernel(
         gated(1)
         scatter(0, 2, 1)
         quantize(2, 4, 14 * KIB)
-        second_layer(2, "g")
-        second_layer(3, "h")
+        second_layer_half(2, 0, "g")
+        second_layer_half(2, 1, "h")
         scatter(1, 2, 0, True)
-        gated(2)
-        gated_half(3, 0)
-        gated_half(3, 1)
+        gated_pair(2, 0)
+        gated_pair(2, 1)
         scatter(2, 4, 0, True)
         scatter(2, 4, 1)
         base0 = frozen(0, 0, T, "e")

@@ -233,7 +233,7 @@ def tile_moe_dyl_gelu_kernel(
             for m in (m0, m0 + 1):
                 part["gy", m] = (pair, P * (m - m0))
         gather("xw", 0, 4)
-        gather("was", 0, 2, 8 * KIB)
+        gather("was", 0, 3)
         gather("xs", 0, 4)
         gather("waw", 0, 1, 0)
         first_layer(0, "a", 9 * KIB)
@@ -242,14 +242,14 @@ def tile_moe_dyl_gelu_kernel(
         turn(0, "c")
         turn(1, "d")
         gather("waw", 2, 3)
-        gather("was", 2, 4, 0)
-        gather("waw", 3, 4, 2 * KIB)
+        gather("was", 3, 4, 0)
+        gather("waw", 3, 4, 2 * KIB + 512)
         first_layer(2, "b")
         first_layer(3, "c", 12 * KIB - 256)
-        gather("wbs", 0, 2, 8 * KIB)
+        gather("wbs", 0, 2, 2 * KIB)
         gather("wbw", 0, 1, 9 * KIB)
         quantize(0, 2, 14 * KIB)
-        gather("wbw", 1, 4, 2 * KIB)
+        gather("wbw", 1, 4, 2 * KIB + 512)
         turn(2, "a")
         turn(3, "f")
         second_layer(0, "b")

@@ -226,7 +226,8 @@ def tile_moe_dyl_gelu_kernel(
         load_scales(wbs, wb_scales, WB_ROW, nc.gpsimd)
         nc.sync.dma_start(out=gate_sb[:], in_=gate)
 
-        new("h", 0, 2, H, BF16)
+        new("h", 0, 1, H, BF16, 18 * KIB)
+        new("h", 1, 2, H, BF16)
         new("h", 2, 4, H, BF16)
         for m0 in (0, 2):
             pair = sb("gy%d" % m0, 2 * N, F32)
@@ -239,39 +240,40 @@ def tile_moe_dyl_gelu_kernel(
         first_layer(0, "a", 9 * KIB)
         gather("waw", 1, 2, 2 * KIB)
         first_layer(1, "b")
+        gather("waw", 2, 3)
+        first_layer(2, "g", 16 * KIB)
         turn(0, "c")
         turn(1, "d")
-        gather("waw", 2, 3)
         gather("was", 3, 4, 0)
         gather("waw", 3, 4, 2 * KIB + 512)
-        first_layer(2, "b")
-        first_layer(3, "c", 12 * KIB - 256)
+        first_layer(3, "b", 12 * KIB - 256)
         gather("wbs", 0, 2, 2 * KIB)
         gather("wbw", 0, 1, 9 * KIB)
-        quantize(0, 2, 14 * KIB)
-        gather("wbw", 1, 4, 2 * KIB + 512)
+        quantize(0, 1)
+        gather("wbw", 1, 4, 18 * KIB)
+        quantize(1, 2, 14 * KIB)
         turn(2, "a")
+        base0 = frozen(0, 0, T, "c")
+        base_sb = sb("base_sb", SPLIT, F32, 16 * KIB)
+        nc.scalar.copy(out=base_sb[:], in_=base0[:, 0:SPLIT])
+        second_layer(0, "g")
         turn(3, "f")
-        second_layer(0, "b")
         placed = [sb("placed%d" % c, T, F32, (10 + 2 * c) * KIB) for c in range(2)]
         gated(0)
         scatter(0, 1, 0)
         gather("wbs", 2, 4, 9 * KIB)
-        second_layer(1, "c")
+        second_layer(1, "b")
+        base1 = frozen(1, 0, T, "f")
         gated(1)
         scatter(0, 2, 1)
         quantize(2, 4, 14 * KIB)
-        second_layer_half(2, 0, "g")
-        second_layer_half(2, 1, "h")
+        second_layer_half(2, 0, "d")
+        second_layer_half(2, 1, "e")
         scatter(1, 2, 0, True)
         gated_pair(2, 0)
         gated_pair(2, 1)
         scatter(2, 4, 0, True)
         scatter(2, 4, 1)
-        base0 = frozen(0, 0, T, "e")
-        base_sb = sb("base_sb", SPLIT, F32, 14 * KIB)
-        nc.scalar.copy(out=base_sb[:], in_=base0[:, 0:SPLIT])
-        base1 = frozen(1, 0, T, "d")
         finish(0, SPLIT, T, base0, nc.sync)
         finish(0, 0, SPLIT, base_sb, nc.scalar, nc.gpsimd)
         finish(1, 0, T // 2, base1, nc.sync)

@@ -237,7 +237,7 @@ def tile_moe_dyl_gelu_kernel(
         gather("was", 0, 3)
         gather("xs", 0, 4)
         gather("waw", 0, 1, 0)
-        first_layer(0, "a", 9 * KIB)
+        first_layer(0, "a", 7 * KIB)
         gather("waw", 1, 2, 2 * KIB)
         first_layer(1, "b")
         gather("waw", 2, 3)
@@ -248,20 +248,20 @@ def tile_moe_dyl_gelu_kernel(
         gather("waw", 3, 4, 2 * KIB + 512)
         first_layer(3, "b", 12 * KIB - 256)
         gather("wbs", 0, 2, 2 * KIB)
-        gather("wbw", 0, 1, 9 * KIB)
+        gather("wbw", 0, 2, 7 * KIB)
         quantize(0, 1)
-        gather("wbw", 1, 4, 18 * KIB)
         quantize(1, 2, 14 * KIB)
+        gather("wbs", 2, 4, 18 * KIB)
         turn(2, "a")
         base0 = frozen(0, 0, T, "c")
         base_sb = sb("base_sb", SPLIT, F32, 16 * KIB)
         nc.scalar.copy(out=base_sb[:], in_=base0[:, 0:SPLIT])
         second_layer(0, "g")
         turn(3, "f")
-        placed = [sb("placed%d" % c, T, F32, (10 + 2 * c) * KIB) for c in range(2)]
+        placed = [sb("placed0", T, F32, 10 * KIB), sb("placed1", T, F32)]
         gated(0)
         scatter(0, 1, 0)
-        gather("wbs", 2, 4, 9 * KIB)
+        gather("wbw", 2, 4, 12 * KIB)
         second_layer(1, "b")
         base1 = frozen(1, 0, T, "f")
         gated(1)

from contextlib import ExitStack

import concourse.mybir as mybir
from concourse.masks import make_identity

K, T, E, B, H, N = 512, 512, 4, 4, 512, 256
P = 128
FLOPS = 2 * K * N * T + 2 * K * H * T + 2 * H * N * T

F32 = mybir.dt.float32
BF16 = mybir.dt.bfloat16
I32 = mybir.dt.int32
U32 = mybir.dt.uint32
U16 = mybir.dt.uint16
U8 = mybir.dt.uint8
FP8X4 = mybir.dt.float8_e4m3fn_x4
FP4X4 = mybir.dt.float4_e2m1fn_x4
GELU = mybir.ActivationFunctionType.Gelu_apprx_tanh
COPY = mybir.ActivationFunctionType.Copy
MULT = mybir.AluOpType.mult
ADD = mybir.AluOpType.add

WA_ROW = 4
WB_ROW = 8
TOKEN_WINDOW = 704
WA_FIRST = 1280
SPLIT = 256
KIB = 1024


def tile_moe_dyl_gelu_kernel(
    tc, x_words, x_scales, w_words, w_scales, wa_words, wa_scales, wb_words, wb_scales, gate, offs, offs2, offs3, out
):
    nc = tc.nc
    with ExitStack() as ctx:
        keep = ctx.enter_context(tc.tile_pool(name="keep", bufs=1))
        shared = ctx.enter_context(tc.tile_pool(name="shared", bufs=1))
        psum = ctx.enter_context(tc.psum_pool(name="psum", bufs=1))

        def sb(name, cols, dtype, at=None):
            if at is None:
                return keep.tile([P, cols], dtype, name=name, align_bytes=64)
            return shared.tile([P, cols], dtype, name=name, align_bytes=64, offset=at)

        def bank(name, slot):
            return psum.tile([P, 512], F32, name=name, tag=slot)

        tok_list = sb("tok_list", T // 16, U16)
        wa_list = sb("wa_list", B * H // 16, U16)
        wb_list = sb("wb_list", B * N // 16, U16)
        xw, xs = sb("xw", TOKEN_WINDOW, I32), sb("xs", TOKEN_WINDOW, U8)
        waw, was = sb("waw", E * H, I32), sb("was", E * H, U8)
        wbw, wbs = sb("wbw", E * N, I32), sb("wbs", E * N, U8)
        ww, ws = sb("ww", 2 * N, U8), sb("ws", N, U8)
        gate_sb = sb("gate_sb", T, F32)
        ident = sb("ident", P, F32)

        def load_words(tile, words, lo, hi, queue=nc.sync):
            queue.dma_start(out=tile[:, lo:hi], in_=words[0, :, lo:hi, :].rearrange("p c d -> p (c d)").bitcast(I32))

        def load_scales(tile, scales, row, queue=nc.sync):
            for r in range(4):
                queue.dma_start(
                    out=tile[row + r : P : 32, 0 : scales.shape[2]].bitcast(I32), in_=scales[0, r:16:4, :].bitcast(I32)
                )

        sources = {
            "xw": (xw[:].bitcast(U32), tok_list, P, U32),
            "xs": (xs[:], tok_list, P, U8),
            "waw": (waw[:].bitcast(U32), wa_list, H, U32),
            "was": (was[:], wa_list, H, U8),
            "wbw": (wbw[:].bitcast(U32), wb_list, N, U32),
            "wbs": (wbs[:], wb_list, N, U8),
        }
        part = {}

        def new(kind, m0, m1, width, dtype, at=None):
            tile = sb("%s_%d" % (kind, m0), width * (m1 - m0), dtype, at)
            for m in range(m0, m1):
                part[kind, m] = (tile, width * (m - m0))
            return tile

        def view(kind, m, lo, hi, row=0):
            tile, first = part[kind, m]
            return tile[row:P, first + lo : first + hi]

        def gather(kind, m0, m1, at=None):
            window, lst, width, dtype = sources[kind]
            tile = new(kind + "g", m0, m1, width, dtype, at)
            nc.vector.tensor_copy(out=tile[:], in_=window.indirect(lst[:, width * m0 // 16 : width * m1 // 16]))

        def first_layer(m, slot, rows_at=None, first_rows_at=None):
            h_ps = bank("h_ps%d" % m, slot)
            nc.tensor.matmul_mx(
                out=h_ps[:],
                lhsT=view("xwg", m, 0, P).bitcast(FP8X4), lhsT_scale=view("xsg", m, 0, P),
                rhs=view("wawg", m, 0, H).bitcast(FP8X4), rhs_scale=view("wasg", m, 0, H, WA_ROW),
                start=True, stop=True,
            )
            for u in range(2):
                rows = new("rows%d" % u, m, m + 1, H // 2, BF16, rows_at if u == 1 else first_rows_at)
                nc.scalar.activation(
                    out=rows[:].rearrange("s (p e) -> s p e", e=2),
                    in_=h_ps[:].rearrange("s (p u e) -> s u p e", u=2, e=2)[:, u],
                    func=GELU,
                )

        def first_layer_whole(m, slot, rows_at):
            h_ps = bank("h_ps%d" % m, slot)
            nc.tensor.matmul_mx(
                out=h_ps[:],
                lhsT=view("xwg", m, 0, P).bitcast(FP8X4), lhsT_scale=view("xsg", m, 0, P),
                rhs=view("wawg", m, 0, H).bitcast(FP8X4), rhs_scale=view("wasg", m, 0, H, WA_ROW),
                start=True, stop=True,
            )
            rows = new("rows", m, m + 1, H, BF16, rows_at)
            nc.scalar.activation(
                out=rows[:].rearrange("s (u p e) -> s u p e", u=2, e=2),
                in_=h_ps[:].rearrange("s (p u e) -> s u p e", u=2, e=2),
                func=GELU,
            )
            for u in range(2):
                part["rows%d" % u, m] = (rows, N * u)

        def turn(m, slot):
            t_ps = bank("t_ps%d" % m, slot)
            for u in range(2):
                nc.tensor.transpose(t_ps[:, P * u : P * u + P], view("rows%d" % u, m, 0, H // 2).bitcast(F32), ident[:])
            nc.scalar.copy(
                out=view("h", m, 0, H).bitcast(F32).rearrange("p (s u) -> p s u", u=2),
                in_=t_ps[:, 0 : 2 * P].rearrange("p (u s) -> p s u", u=2),
            )

        def quantize(m0, m1, at=None, scales_at=None):
            hq = new("hq", m0, m1, P, U32, at)
            hs = new("hs", m0, m1, P, U8, scales_at)
            nc.vector.quantize_mx(out=hq[:].bitcast(FP8X4), scales=hs[:], in_=view("h", m0, 0, H * (m1 - m0)))

        def second_layer(m, slot):
            y_ps = bank("y_ps%d" % m, slot)
            for c in range(2):
                nc.tensor.matmul_mx(
                    out=y_ps[:, P * c : P * c + P],
                    lhsT=view("wbwg", m, P * c, P * c + P).bitcast(FP8X4),
                    lhsT_scale=view("wbsg", m, P * c, P * c + P, WB_ROW),
                    rhs=view("hq", m, 0, P).bitcast(FP8X4), rhs_scale=view("hs", m, 0, P),
                    start=True, stop=True,
                )
            part["y", m] = y_ps

        def second_layer_half(m0, c, slot):
            y_ps = bank("y_ps%d_%d" % (m0, c), slot)
            for m in (m0, m0 + 1):
                nc.tensor.matmul_mx(
                    out=y_ps[:, P * (m - m0) : P * (m - m0) + P],
                    lhsT=view("wbwg", m, P * c, P * c + P).bitcast(FP8X4),
                    lhsT_scale=view("wbsg", m, P * c, P * c + P, WB_ROW),
                    rhs=view("hq", m, 0, P).bitcast(FP8X4), rhs_scale=view("hs", m, 0, P),
                    start=True, stop=True,
                )
            part["y", m0, c] = y_ps

        def gated_pair(m0, c):
            nc.vector.tensor_tensor(
                out=view("gy", m0, N * c, N * c + N), in0=part["y", m0, c][:, 0:N],
                in1=gate_sb[:, P * m0 : P * m0 + N], op=MULT,
            )

        def gated(m):
            pair, first = part["gy", m]
            nc.vector.tensor_tensor(
                out=pair[:].rearrange("p (c s) -> p c s", c=2)[:, :, first : first + P],
                in0=part["y", m][:, 0:N].rearrange("p (c s) -> p c s", c=2),
                in1=gate_sb[:, P * m : P * m + P].unsqueeze(1).to_broadcast([P, 2, P]),
                op=MULT,
            )

        def gated_half(m, c):
            pair, first = part["gy", m]
            at = N * c + first
            nc.vector.tensor_tensor(
                out=pair[:, at : at + P], in0=part["y", m][:, P * c : P * c + P], in1=gate_sb[:, P * m : P * m + P], op=MULT
            )

        def scatter(m0, m1, c, on_vector=False):
            target = placed[c][:].indirect(tok_list[:, P * m0 // 16 : P * m1 // 16])
            values = view("gy", m0, N * c, N * c + P * (m1 - m0))
            if on_vector:
                nc.vector.tensor_copy(out=target, in_=values)
            else:
                nc.scalar.activation(out=target, in_=values, func=COPY)

        def frozen(c, lo, hi, slot):
            base_ps = bank("base%d_%d" % (c, lo), slot)
            nc.tensor.matmul_mx(
                out=base_ps[:, lo:hi],
                lhsT=ww[:, 2 * P * c : 2 * P * c + 2 * P].bitcast(FP4X4), lhsT_scale=ws[:, P * c : P * c + P],
                rhs=xw[:, lo:hi].bitcast(FP8X4), rhs_scale=xs[:, lo:hi],
                start=True, stop=True,
            )
            return base_ps

        def finish(c, lo, hi, base, queue, engine=nc.vector):
            res = sb("res%d_%d" % (c, lo), hi - lo, F32)
            engine.tensor_tensor(out=res[:], in0=base[:, lo:hi], in1=placed[c][:, lo:hi], op=ADD)
            queue.dma_start(out=out[P * c : P * c + P, lo:hi], in_=res[:])

        nc.gpsimd.memset(wbs[:].bitcast(I32), 0)
        for plane in (was, xs, ws):
            nc.vector.memset(plane[:].bitcast(I32), 0)
        nc.vector.memset(xw[:, T:TOKEN_WINDOW], 0)
        nc.vector.memset(ident[:], 0.0)
        make_identity(nc, ident[:], nomemset=True)

        load_words(xw, x_words, 0, T, nc.scalar)
        nc.sync.dma_start(tok_list[:], offs)
        nc.sync.dma_start(wa_list[:], offs2)
        load_scales(was, wa_scales, WA_ROW)
        load_words(waw, wa_words, 0, WA_FIRST)
        load_scales(xs, x_scales, 0)
        load_words(waw, wa_words, WA_FIRST, E * H)
        nc.gpsimd.dma_start(out=ww[:].bitcast(I32), in_=w_words[0].bitcast(I32))
        load_scales(ws, w_scales, 0)
        nc.sync.dma_start(wb_list[:], offs3)
        load_words(wbw, wb_words, 0, E * N)
        load_scales(wbs, wb_scales, WB_ROW, nc.gpsimd)
        nc.sync.dma_start(out=gate_sb[:], in_=gate)

        new("h", 0, 1, H, BF16, 18 * KIB)
        new("h", 1, 2, H, BF16)
        new("h", 2, 4, H, BF16)
        for m0 in (0, 2):
            pair = sb("gy%d" % m0, 2 * N, F32)
            for m in (m0, m0 + 1):
                part["gy", m] = (pair, P * (m - m0))
        gather("xw", 0, 4)
        gather("was", 0, 3)
        gather("xs", 0, 4)
        gather("waw", 0, 1, 0)
        first_layer(0, "a", 7 * KIB)
        gather("waw", 1, 2, 2 * KIB)
        first_layer(1, "b")
        gather("waw", 2, 3)
        first_layer(2, "g", 16 * KIB)
        turn(0, "c")
        turn(1, "d")
        gather("was", 3, 4, 0)
        gather("waw", 3, 4, 2 * KIB + 512)
        first_layer(3, "b", 12 * KIB - 256)
        gather("wbs", 0, 2, 2 * KIB)
        gather("wbw", 0, 2, 7 * KIB)
        quantize(0, 1)
        quantize(1, 2, 14 * KIB)
        gather("wbs", 2, 4, 18 * KIB)
        turn(2, "a")
        base0 = frozen(0, 0, T, "c")
        base_sb = sb("base_sb", SPLIT, F32, 16 * KIB)
        nc.scalar.copy(out=base_sb[:], in_=base0[:, 0:SPLIT])
        second_layer(0, "g")
        turn(3, "f")
        placed = [sb("placed0", T, F32, 10 * KIB), sb("placed1", T, F32)]
        gated(0)
        scatter(0, 1, 0)
        gather("wbw", 2, 4, 12 * KIB)
        second_layer(1, "b")
        base1 = frozen(1, 0, T, "f")
        gated(1)
        scatter(0, 2, 1)
        quantize(2, 4, 14 * KIB)
        second_layer_half(2, 0, "d")
        second_layer_half(2, 1, "e")
        scatter(1, 2, 0, True)
        gated_pair(2, 0)
        gated_pair(2, 1)
        scatter(2, 4, 0, True)
        scatter(2, 4, 1)
        finish(0, SPLIT, T, base0, nc.sync)
        finish(0, 0, SPLIT, base_sb, nc.scalar, nc.gpsimd)
        finish(1, 0, T // 2, base1, nc.sync)
        finish(1, T // 2, T, base1, nc.sync)
